import numpy as np
import ml_dtypes


def mxq(x, axis, fmt="e4m3"):
    dtype, down = {"e4m3": (ml_dtypes.float8_e4m3fn, 7), "e5m2": (ml_dtypes.float8_e5m2, 14)}[fmt]
    v = np.moveaxis(np.asarray(x, np.float32).astype(ml_dtypes.bfloat16).astype(np.float64), axis, -1)
    blocks = v.reshape(v.shape[:-1] + (-1, 32))
    amax = np.abs(blocks).max(-1, keepdims=True)
    byte = np.maximum(np.where(amax > 0, np.frexp(amax)[1] - 1 + 127, 0) - down, 1)
    scale = np.exp2(byte - 127.0)
    codes = (blocks / scale).astype(np.float32).astype(dtype).astype(np.float64)
    return np.moveaxis((codes * scale).reshape(v.shape), -1, axis)


WIDE = False


def mx_kscale(k):
    if not WIDE:
        return np.ones(k)
    levels = np.array([10, -10, 5, -5, 0])
    if k % 512:
        return np.exp2(np.random.permutation(np.resize(levels, k // 32))).repeat(32)
    a = np.empty((k // 512, 16))
    for p in range(k // 512):
        a[p, :8] = np.random.permutation(np.resize(levels, 8))
        for g in range(8):
            far = levels[np.abs(levels - a[p, g]) >= 10]
            a[p, g + 8] = far[np.random.randint(len(far))]
    return np.exp2(a.ravel()).repeat(32)


def f64(x):
    return np.asarray(x).astype(np.float64)


def striped(idx):
    return np.tile(idx.reshape(-1, 16).T, (8, 1)).astype(np.uint16)


def unstriped(offs):
    return offs[:16].T.reshape(-1).astype(np.int64)


def striped8(idx):
    return np.concatenate([x.reshape(-1, 16).T for x in idx]).astype(np.uint16)


def runs(offs, k):
    lists = np.stack([offs[16 * r : 16 * r + 16].T.reshape(-1) for r in range(8)]).astype(np.int64)
    return lists[np.arange(k) % 512 // 64]


def pack_weight(w):
    k, n = w.shape
    w = f64(np.asarray(w, np.float32).astype(ml_dtypes.bfloat16)).reshape(k // 32, 32, n)
    amax = np.abs(w).max(1)
    byte = np.clip(np.where(amax > 0, np.frexp(amax)[1] - 1 + 127 - 7, 1), 1, 254)
    scaled = (w * np.exp2(127.0 - byte)[:, None, :]).reshape(k, n).astype(np.float32)
    words = np.ascontiguousarray(scaled.reshape(k // 512, 128, 4, n).transpose(0, 1, 3, 2)).astype(ml_dtypes.float8_e4m3fn).view(np.uint8)
    return words, np.ascontiguousarray(byte.astype(np.uint8).reshape(k // 512, 16, n))


def unpack_weight(words, scales):
    g, p, n, _ = words.shape
    vals = np.ascontiguousarray(words).view(ml_dtypes.float8_e4m3fn).astype(np.float64) * np.repeat(np.exp2(scales.astype(np.float64) - 127.0), 8, axis=1)[..., None]
    return vals.transpose(0, 1, 3, 2).reshape(g * 512, n)


K, T, S, N, H = 512, 2048, 512, 512, 512


def setup_inputs():
    n = np.random.standard_normal
    s = mx_kscale(K)[:, None]
    u = mx_kscale(H)
    packed_xT = pack_weight(n((K, T)) * s)
    return {
        "x_words": packed_xT[0],
        "x_scales": packed_xT[1],
        "w1": (n((K, H)) / np.sqrt(K) / s * u).astype(np.float32),
        "up": np.clip(n((H, S)), 0.25, 1.0).astype(np.float32),
        "w2": (n((H, N)) / np.sqrt(H) / u[:, None]).astype(np.float32),
        "offs": striped(np.random.permutation(T)[:S]),
        "mate": striped8(np.stack([np.random.permutation(S) for _ in range(8)])),
    }


def reference(x_words, x_scales, w1, up, w2, offs, mate):
    xq = unpack_weight(x_words, x_scales)[:, unstriped(offs)]
    y = mxq(f64(w1), 0, "e4m3").T @ xq
    o = y[np.arange(H)[:, None], runs(mate, H)]
    lo = np.minimum(y, o)
    z = lo + f64(up) * (np.maximum(y, o) - lo)
    return mxq(f64(w2), 0, "e4m3").T @ mxq(z, 0, "e4m3")

@@ -1,0 +1,171 @@
+from contextlib import ExitStack
+
+import concourse.mybir as mybir
+
+K, T, S, N, H = 512, 2048, 512, 512, 512
+FLOPS = 2 * K * H * S + 2 * H * N * S
+
+F32 = mybir.dt.float32
+BF16 = mybir.dt.bfloat16
+I32 = mybir.dt.int32
+U32 = mybir.dt.uint32
+U16 = mybir.dt.uint16
+U8 = mybir.dt.uint8
+FP8X4 = mybir.dt.float8_e4m3fn_x4
+ALU = mybir.AluOpType
+ACT = mybir.ActivationFunctionType
+
+P = 128
+PACK = 4
+HALF = S // 2
+CHUNKS = [(0, 256), (256, 128), (384, 128)]
+
+
+def tile_picked_cmpex_none_p_kernel(tc, x_words, x_scales, w1, up, w2, offs, mate, out):
+    nc = tc.nc
+    with ExitStack() as ctx:
+        keep = ctx.enter_context(tc.tile_pool(name="keep", bufs=1))
+        psum = ctx.enter_context(tc.psum_pool(name="psum", bufs=1))
+
+        offs_sb = keep.tile([P, S // 16], U16, name="offs_sb")
+        nc.sync.dma_start(offs_sb[:], offs)
+        w1_raw = keep.tile([P, PACK, H], F32, name="w1_raw", tag="raw")
+        nc.sync.dma_start(w1_raw[:], w1.rearrange("(p j) c -> p j c", j=PACK))
+        x_table = keep.tile([P, T], U32, name="x_table", align_bytes=64)
+        nc.sync.dma_start(x_table[:].bitcast(I32), x_words[0].rearrange("p n t -> p (n t)").bitcast(I32))
+        mate_sb = keep.tile([P, S // 16], U16, name="mate_sb")
+        nc.sync.dma_start(mate_sb[:], mate)
+
+        scale_table = keep.tile([P, T], U8, name="scale_table", align_bytes=64)
+        nc.vector.memset(scale_table[:].bitcast(I32), 0)
+        for q in range(4):
+            nc.scalar.dma_start(scale_table[32 * q : 32 * q + 4, :].bitcast(I32), x_scales[0, 4 * q : 4 * q + 4, :].bitcast(I32))
+        x_sc = keep.tile([P, S], U8, name="x_sc", align_bytes=64)
+        nc.vector.tensor_copy(x_sc[:], scale_table[:].indirect(offs_sb[:]))
+
+        w1_codes, w1_sc = [], []
+        w1_bf = []
+        for u in range(2):
+            bf = keep.tile([P, 2, P, PACK], BF16, name="w1_bf%d" % u, align_bytes=64)
+            nc.vector.tensor_copy(
+                bf[:].rearrange("p e m j -> p m j e"),
+                w1_raw[:].rearrange("p j (m t) -> p m j t", t=PACK)[:, :, :, 2 * u : 2 * u + 2],
+            )
+            w1_bf.append(bf)
+        for u in range(2):
+            codes = keep.tile([P, 2 * P], U32, name="w1_codes%d" % u, align_bytes=64)
+            sc = keep.tile([P, 2 * P], U8, name="w1_sc%d" % u, align_bytes=64)
+            nc.vector.quantize_mx(out=codes[:].bitcast(FP8X4), scales=sc[:], in_=w1_bf[u][:].rearrange("p e m j -> p (e m j)"))
+            w1_codes.append(codes)
+            w1_sc.append(sc)
+
+        late = keep.tile([P, 2 * PACK, H], F32, name="late", tag="raw")
+        nc.sync.dma_start(late[:, 0:PACK, :], up.rearrange("(p t) s -> p t s", t=PACK))
+        nc.sync.dma_start(late[:, PACK : 2 * PACK, :], w2.rearrange("(p t) n -> p t n", t=PACK))
+
+        x_codes = []
+        for h in range(2):
+            g = keep.tile([P, HALF], U32, name="x_codes%d" % h, align_bytes=64)
+            nc.vector.tensor_copy(g[:], x_table[:].indirect(offs_sb[:, 16 * h : 16 * h + 16]))
+            x_codes.append(g)
+
+        y_plain = keep.tile([P, PACK, S], F32, name="y_plain")
+        diff = keep.tile([P, PACK, S], F32, name="diff")
+        for t in range(PACK):
+            cols = slice(P * (t % 2), P * (t % 2) + P)
+            window = keep.tile([P, S], F32, name="y_window%d" % t)
+            for h in range(2):
+                hs = slice(HALF * h, HALF * h + HALF)
+                bank = psum.tile([P, HALF], F32, name="y_bank", tag="bank%d" % (2 * t + h))
+                nc.tensor.matmul_mx(
+                    out=bank[:],
+                    lhsT=w1_codes[t // 2][:, cols].bitcast(FP8X4),
+                    lhsT_scale=w1_sc[t // 2][:, cols],
+                    rhs=x_codes[h][:].bitcast(FP8X4),
+                    rhs_scale=x_sc[:, hs],
+                    start=True,
+                    stop=True,
+                )
+                nc.scalar.copy(window[:, hs], bank[:])
+                nc.scalar.copy(y_plain[:, t, hs], bank[:])
+            for h in range(2):
+                hs = slice(HALF * h, HALF * h + HALF)
+                nc.vector.tensor_tensor(diff[:, t, hs], window[:].indirect(mate_sb[:, 16 * h : 16 * h + 16]), y_plain[:, t, hs], ALU.subtract)
+
+        gaps = []
+        for c, (c0, n) in enumerate(CHUNKS):
+            gap = keep.tile([P, PACK, n], F32, name="gap%d" % c)
+            nc.scalar.activation(gap[:], diff[:, :, c0 : c0 + n], ACT.Abs)
+            gaps.append(gap)
+
+        w2_bf = keep.tile([P, N, PACK], BF16, name="w2_bf", align_bytes=64)
+        for h in range(2):
+            ns = slice(HALF * h, HALF * h + HALF)
+            nc.scalar.copy(
+                w2_bf[:, ns, :].rearrange("p (c i) t -> p c t i", i=2),
+                late[:, PACK : 2 * PACK, ns].rearrange("p t (c i) -> p c t i", i=2),
+            )
+        w2_codes = keep.tile([P, N], U32, name="w2_codes", align_bytes=64)
+        w2_sc = keep.tile([P, N], U8, name="w2_sc", align_bytes=64)
+
+        def lower(c):
+            c0, n = CHUNKS[c]
+            lo = keep.tile([P, PACK, n], F32, name="lo%d" % c)
+            nc.vector.scalar_tensor_tensor(lo[:], diff[:, :, c0 : c0 + n], 0.0, y_plain[:, :, c0 : c0 + n], ALU.min, ALU.add)
+            return lo
+
+        def share(c):
+            c0, n = CHUNKS[c]
+            part = keep.tile([P, PACK, n], F32, name="part%d" % c)
+            nc.vector.tensor_tensor(part[:], gaps[c][:], late[:, 0:PACK, c0 : c0 + n], ALU.mult)
+            return part
+
+        def mix(c, lo, part):
+            n = CHUNKS[c][1]
+            z_bf = keep.tile([P, n, PACK], BF16, name="z_bf%d" % c, align_bytes=64)
+            nc.vector.tensor_tensor(
+                z_bf[:].rearrange("p (c i) t -> p c t i", i=2),
+                lo[:].rearrange("p t (c i) -> p c t i", i=2),
+                part[:].rearrange("p t (c i) -> p c t i", i=2),
+                ALU.add,
+            )
+            return z_bf
+
+        def finish(c, z_bf, bank0):
+            c0, n = CHUNKS[c]
+            codes = keep.tile([P, n], U32, name="z_codes%d" % c, align_bytes=64)
+            sc = keep.tile([P, n], U8, name="z_sc%d" % c, align_bytes=64)
+            nc.vector.quantize_mx(out=codes[:].bitcast(FP8X4), scales=sc[:], in_=z_bf[:].rearrange("p n t -> p (n t)"))
+            for b in range(2):
+                bank = psum.tile([P, 2, n], F32, name="o_bank", tag="bank%d" % (bank0 + b))
+                for e in range(2):
+                    cols = slice(P * (2 * b + e), P * (2 * b + e) + P)
+                    nc.tensor.matmul_mx(
+                        out=bank[:, e, :],
+                        lhsT=w2_codes[:, cols].bitcast(FP8X4),
+                        lhsT_scale=w2_sc[:, cols],
+                        rhs=codes[:].bitcast(FP8X4),
+                        rhs_scale=sc[:],
+                        start=True,
+                        stop=True,
+                    )
+                res = keep.tile([P, 2, n], F32, name="res%d_%d" % (c, b))
+                if c == len(CHUNKS) - 1 and b == 1:
+                    nc.vector.tensor_copy(res[:], bank[:])
+                else:
+                    nc.scalar.copy(res[:], bank[:])
+                nc.sync.dma_start(out[2 * P * b : 2 * P * (b + 1), c0 : c0 + n].rearrange("(e p) s -> p e s", p=P), res[:])
+
+        lo0 = lower(0)
+        part0 = share(0)
+        lo1 = lower(1)
+        z0 = mix(0, lo0, part0)
+        part1 = share(1)
+        nc.vector.quantize_mx(out=w2_codes[:].bitcast(FP8X4), scales=w2_sc[:], in_=w2_bf[:].rearrange("p n t -> p (n t)"))
+        finish(0, z0, 0)
+        lo2 = lower(2)
+        z1 = mix(1, lo1, part1)
+        part2 = share(2)
+        finish(1, z1, 2)
+        z2 = mix(2, lo2, part2)
+        finish(2, z2, 4)

@@ -18,6 +18,7 @@ ACT = mybir.ActivationFunctionType
 P = 128
 PACK = 4
 HALF = S // 2
+W1_PIECES = [(0, 256), (256, 128), (384, 128)]
 CHUNKS = [(0, 256), (256, 128), (384, 128)]
 
 
@@ -29,73 +30,97 @@ def tile_picked_cmpex_none_p_kernel(tc, x_words, x_scales, w1, up, w2, offs, mat
 
         offs_sb = keep.tile([P, S // 16], U16, name="offs_sb")
         nc.sync.dma_start(offs_sb[:], offs)
-        w1_raw = keep.tile([P, PACK, H], F32, name="w1_raw", tag="raw")
-        nc.sync.dma_start(w1_raw[:], w1.rearrange("(p j) c -> p j c", j=PACK))
+        scale_table = keep.tile([P, T], U8, name="scale_table", align_bytes=64)
+        nc.vector.memset(scale_table[:].bitcast(I32), 0)
         x_table = keep.tile([P, T], U32, name="x_table", align_bytes=64)
-        nc.sync.dma_start(x_table[:].bitcast(I32), x_words[0].rearrange("p n t -> p (n t)").bitcast(I32))
+        x_view = x_words[0].rearrange("p n t -> p (n t)").bitcast(I32)
+        nc.sync.dma_start(x_table[:, 0 : T // 2].bitcast(I32), x_view[:, 0 : T // 2])
+        for q in range(4):
+            nc.sync.dma_start(scale_table[32 * q : 32 * q + 4, :].bitcast(I32), x_scales[0, 4 * q : 4 * q + 4, :].bitcast(I32))
+        nc.sync.dma_start(x_table[:, T // 2 : T].bitcast(I32), x_view[:, T // 2 : T])
+        w1_view = w1.rearrange("(p j) c -> p j c", j=PACK)
+        w1_raw = []
+        for i, (c0, n) in enumerate(W1_PIECES):
+            raw = keep.tile([P, PACK, n], F32, name="w1_raw", tag="raw%d" % i)
+            nc.sync.dma_start(raw[:], w1_view[:, :, c0 : c0 + n])
+            w1_raw.append(raw)
         mate_sb = keep.tile([P, S // 16], U16, name="mate_sb")
         nc.sync.dma_start(mate_sb[:], mate)
 
-        scale_table = keep.tile([P, T], U8, name="scale_table", align_bytes=64)
-        nc.vector.memset(scale_table[:].bitcast(I32), 0)
-        for q in range(4):
-            nc.scalar.dma_start(scale_table[32 * q : 32 * q + 4, :].bitcast(I32), x_scales[0, 4 * q : 4 * q + 4, :].bitcast(I32))
         x_sc = keep.tile([P, S], U8, name="x_sc", align_bytes=64)
         nc.vector.tensor_copy(x_sc[:], scale_table[:].indirect(offs_sb[:]))
+        x_codes = keep.tile([P, S], U32, name="x_codes", align_bytes=64)
+        nc.vector.tensor_copy(x_codes[:], x_table[:].indirect(offs_sb[:]))
 
-        w1_codes, w1_sc = [], []
-        w1_bf = []
-        for u in range(2):
-            bf = keep.tile([P, 2, P, PACK], BF16, name="w1_bf%d" % u, align_bytes=64)
-            nc.vector.tensor_copy(
-                bf[:].rearrange("p e m j -> p m j e"),
-                w1_raw[:].rearrange("p j (m t) -> p m j t", t=PACK)[:, :, :, 2 * u : 2 * u + 2],
+        w1_bf = [keep.tile([P, 2, P, PACK], BF16, name="w1_bf%d" % u, align_bytes=64) for u in range(2)]
+        w1_codes = [keep.tile([P, 2 * P], U32, name="w1_codes%d" % u, align_bytes=64) for u in range(2)]
+        w1_sc = [keep.tile([P, 2 * P], U8, name="w1_sc%d" % u, align_bytes=64) for u in range(2)]
+
+        def cast_w1(i, u):
+            c0, n = W1_PIECES[i]
+            dst = w1_bf[u][:, :, c0 // PACK : (c0 + n) // PACK, :].rearrange("p e m j -> p m j e")
+            src = w1_raw[i][:].rearrange("p j (m t) -> p m j t", t=PACK)[:, :, :, 2 * u : 2 * u + 2]
+            if i < 2:
+                nc.scalar.copy(dst, src)
+            else:
+                nc.vector.tensor_copy(dst, src)
+
+        def quantize_w1(u, e0, e1):
+            cols = slice(P * e0, P * e1)
+            nc.vector.quantize_mx(
+                out=w1_codes[u][:, cols].bitcast(FP8X4),
+                scales=w1_sc[u][:, cols],
+                in_=w1_bf[u][:, e0:e1, :, :].rearrange("p e m j -> p (e m j)"),
             )
-            w1_bf.append(bf)
+
         for u in range(2):
-            codes = keep.tile([P, 2 * P], U32, name="w1_codes%d" % u, align_bytes=64)
-            sc = keep.tile([P, 2 * P], U8, name="w1_sc%d" % u, align_bytes=64)
-            nc.vector.quantize_mx(out=codes[:].bitcast(FP8X4), scales=sc[:], in_=w1_bf[u][:].rearrange("p e m j -> p (e m j)"))
-            w1_codes.append(codes)
-            w1_sc.append(sc)
+            for i in range(len(W1_PIECES)):
+                cast_w1(i, u)
+            if u == 0:
+                quantize_w1(0, 0, 1)
+        quantize_w1(0, 1, 2)
+        quantize_w1(1, 0, 2)
 
-        late = keep.tile([P, 2 * PACK, H], F32, name="late", tag="raw")
-        nc.sync.dma_start(late[:, 0:PACK, :], up.rearrange("(p t) s -> p t s", t=PACK))
-        nc.sync.dma_start(late[:, PACK : 2 * PACK, :], w2.rearrange("(p t) n -> p t n", t=PACK))
+        up_sb = keep.tile([P, PACK, S], F32, name="up_sb", tag="raw0")
+        nc.sync.dma_start(up_sb[:], up.rearrange("(p t) s -> p t s", t=PACK))
+        w2_raw = keep.tile([P, PACK, N], F32, name="w2_raw", tag="raw1")
+        nc.sync.dma_start(w2_raw[:], w2.rearrange("(p t) n -> p t n", t=PACK))
 
-        x_codes = []
-        for h in range(2):
-            g = keep.tile([P, HALF], U32, name="x_codes%d" % h, align_bytes=64)
-            nc.vector.tensor_copy(g[:], x_table[:].indirect(offs_sb[:, 16 * h : 16 * h + 16]))
-            x_codes.append(g)
-
+        halves = [slice(0, HALF), slice(HALF, S)]
         y_plain = keep.tile([P, PACK, S], F32, name="y_plain")
         diff = keep.tile([P, PACK, S], F32, name="diff")
+        banks = 0
         for t in range(PACK):
             cols = slice(P * (t % 2), P * (t % 2) + P)
-            window = keep.tile([P, S], F32, name="y_window%d" % t)
-            for h in range(2):
-                hs = slice(HALF * h, HALF * h + HALF)
-                bank = psum.tile([P, HALF], F32, name="y_bank", tag="bank%d" % (2 * t + h))
+            window = keep.tile([P, S if t == 0 else 2 * S], F32, name="y_window%d" % t)
+            if t > 0:
+                nc.gpsimd.memset(window[:, S : 2 * S], 0.0)
+            for piece in halves if t == 0 else [slice(0, S)]:
+                n = piece.stop - piece.start
+                bank = psum.tile([P, n], F32, name="y_bank", tag="bank%d" % banks)
+                banks = banks + 1
                 nc.tensor.matmul_mx(
                     out=bank[:],
                     lhsT=w1_codes[t // 2][:, cols].bitcast(FP8X4),
                     lhsT_scale=w1_sc[t // 2][:, cols],
-                    rhs=x_codes[h][:].bitcast(FP8X4),
-                    rhs_scale=x_sc[:, hs],
+                    rhs=x_codes[:, piece].bitcast(FP8X4),
+                    rhs_scale=x_sc[:, piece],
                     start=True,
                     stop=True,
                 )
-                nc.scalar.copy(window[:, hs], bank[:])
-                nc.scalar.copy(y_plain[:, t, hs], bank[:])
-            for h in range(2):
-                hs = slice(HALF * h, HALF * h + HALF)
-                nc.vector.tensor_tensor(diff[:, t, hs], window[:].indirect(mate_sb[:, 16 * h : 16 * h + 16]), y_plain[:, t, hs], ALU.subtract)
+                if t == 0 and piece.start > 0:
+                    nc.vector.tensor_copy(window[:, piece], bank[:])
+                else:
+                    nc.scalar.copy(window[:, piece], bank[:])
+                nc.scalar.copy(y_plain[:, t, piece], bank[:])
+            for piece in halves if t == 0 else [slice(0, S)]:
+                picks = mate_sb[:, piece.start // 16 : piece.stop // 16]
+                nc.vector.tensor_tensor(diff[:, t, piece], window[:].indirect(picks), y_plain[:, t, piece], ALU.subtract)
 
         gaps = []
-        for c, (c0, n) in enumerate(CHUNKS):
-            gap = keep.tile([P, PACK, n], F32, name="gap%d" % c)
-            nc.scalar.activation(gap[:], diff[:, :, c0 : c0 + n], ACT.Abs)
+        for h in range(2):
+            gap = keep.tile([P, PACK, HALF], F32, name="gap%d" % h)
+            nc.scalar.activation(gap[:], diff[:, :, halves[h]], ACT.Abs)
             gaps.append(gap)
 
         w2_bf = keep.tile([P, N, PACK], BF16, name="w2_bf", align_bytes=64)
@@ -103,30 +128,29 @@ def tile_picked_cmpex_none_p_kernel(tc, x_words, x_scales, w1, up, w2, offs, mat
             ns = slice(HALF * h, HALF * h + HALF)
             nc.scalar.copy(
                 w2_bf[:, ns, :].rearrange("p (c i) t -> p c t i", i=2),
-                late[:, PACK : 2 * PACK, ns].rearrange("p t (c i) -> p c t i", i=2),
+                w2_raw[:, :, ns].rearrange("p t (c i) -> p c t i", i=2),
             )
         w2_codes = keep.tile([P, N], U32, name="w2_codes", align_bytes=64)
         w2_sc = keep.tile([P, N], U8, name="w2_sc", align_bytes=64)
 
-        def lower(c):
-            c0, n = CHUNKS[c]
-            lo = keep.tile([P, PACK, n], F32, name="lo%d" % c)
-            nc.vector.scalar_tensor_tensor(lo[:], diff[:, :, c0 : c0 + n], 0.0, y_plain[:, :, c0 : c0 + n], ALU.min, ALU.add)
+        def lower(h):
+            lo = keep.tile([P, PACK, HALF], F32, name="lo%d" % h)
+            nc.vector.scalar_tensor_tensor(lo[:], diff[:, :, halves[h]], 0.0, y_plain[:, :, halves[h]], ALU.min, ALU.add)
             return lo
 
-        def share(c):
-            c0, n = CHUNKS[c]
-            part = keep.tile([P, PACK, n], F32, name="part%d" % c)
-            nc.vector.tensor_tensor(part[:], gaps[c][:], late[:, 0:PACK, c0 : c0 + n], ALU.mult)
+        def share(h):
+            part = keep.tile([P, PACK, HALF], F32, name="part%d" % h)
+            nc.vector.tensor_tensor(part[:], gaps[h][:], up_sb[:, :, halves[h]], ALU.mult)
             return part
 
         def mix(c, lo, part):
-            n = CHUNKS[c][1]
+            c0, n = CHUNKS[c]
+            cols = slice(c0 % HALF, c0 % HALF + n)
             z_bf = keep.tile([P, n, PACK], BF16, name="z_bf%d" % c, align_bytes=64)
             nc.vector.tensor_tensor(
                 z_bf[:].rearrange("p (c i) t -> p c t i", i=2),
-                lo[:].rearrange("p t (c i) -> p c t i", i=2),
-                part[:].rearrange("p t (c i) -> p c t i", i=2),
+                lo[:, :, cols].rearrange("p t (c i) -> p c t i", i=2),
+                part[:, :, cols].rearrange("p t (c i) -> p c t i", i=2),
                 ALU.add,
             )
             return z_bf
@@ -154,7 +178,8 @@ def tile_picked_cmpex_none_p_kernel(tc, x_words, x_scales, w1, up, w2, offs, mat
                     nc.vector.tensor_copy(res[:], bank[:])
                 else:
                     nc.scalar.copy(res[:], bank[:])
-                nc.sync.dma_start(out[2 * P * b : 2 * P * (b + 1), c0 : c0 + n].rearrange("(e p) s -> p e s", p=P), res[:])
+                queue = nc.scalar if c == len(CHUNKS) - 1 and b == 0 else nc.sync
+                queue.dma_start(out[2 * P * b : 2 * P * (b + 1), c0 : c0 + n].rearrange("(e p) s -> p e s", p=P), res[:])
 
         lo0 = lower(0)
         part0 = share(0)
@@ -163,9 +188,7 @@ def tile_picked_cmpex_none_p_kernel(tc, x_words, x_scales, w1, up, w2, offs, mat
         part1 = share(1)
         nc.vector.quantize_mx(out=w2_codes[:].bitcast(FP8X4), scales=w2_sc[:], in_=w2_bf[:].rearrange("p n t -> p (n t)"))
         finish(0, z0, 0)
-        lo2 = lower(2)
         z1 = mix(1, lo1, part1)
-        part2 = share(2)
+        z2 = mix(2, lo1, part1)
         finish(1, z1, 2)
-        z2 = mix(2, lo2, part2)
         finish(2, z2, 4)

@@ -18,12 +18,12 @@ ACT = mybir.ActivationFunctionType
 P = 128
 PACK = 4
 HALF = S // 2
-W1_PIECES = [(0, 256), (256, 128), (384, 128)]
 CHUNKS = [(0, 256), (256, 128), (384, 128)]
 
 
 def tile_picked_cmpex_none_p_kernel(tc, x_words, x_scales, w1, up, w2, offs, mate, out):
     nc = tc.nc
+    halves = [slice(0, HALF), slice(HALF, S)]
     with ExitStack() as ctx:
         keep = ctx.enter_context(tc.tile_pool(name="keep", bufs=1))
         psum = ctx.enter_context(tc.psum_pool(name="psum", bufs=1))
@@ -32,73 +32,46 @@ def tile_picked_cmpex_none_p_kernel(tc, x_words, x_scales, w1, up, w2, offs, mat
         nc.sync.dma_start(offs_sb[:], offs)
         scale_table = keep.tile([P, T], U8, name="scale_table", align_bytes=64)
         nc.vector.memset(scale_table[:].bitcast(I32), 0)
-        x_table = keep.tile([P, T], U32, name="x_table", align_bytes=64)
-        x_view = x_words[0].rearrange("p n t -> p (n t)").bitcast(I32)
-        nc.sync.dma_start(x_table[:, 0 : T // 2].bitcast(I32), x_view[:, 0 : T // 2])
+        w1_raw = keep.tile([P, PACK, H], F32, name="w1_raw", tag="raw")
+        nc.sync.dma_start(w1_raw[:], w1.rearrange("(p j) c -> p j c", j=PACK))
         for q in range(4):
             nc.sync.dma_start(scale_table[32 * q : 32 * q + 4, :].bitcast(I32), x_scales[0, 4 * q : 4 * q + 4, :].bitcast(I32))
-        nc.sync.dma_start(x_table[:, T // 2 : T].bitcast(I32), x_view[:, T // 2 : T])
-        w1_view = w1.rearrange("(p j) c -> p j c", j=PACK)
-        w1_raw = []
-        for i, (c0, n) in enumerate(W1_PIECES):
-            raw = keep.tile([P, PACK, n], F32, name="w1_raw", tag="raw%d" % i)
-            nc.sync.dma_start(raw[:], w1_view[:, :, c0 : c0 + n])
-            w1_raw.append(raw)
+        x_table = keep.tile([P, T], U32, name="x_table", align_bytes=64)
+        nc.sync.dma_start(x_table[:].bitcast(I32), x_words[0].rearrange("p n t -> p (n t)").bitcast(I32))
         mate_sb = keep.tile([P, S // 16], U16, name="mate_sb")
         nc.sync.dma_start(mate_sb[:], mate)
-
-        x_sc = keep.tile([P, S], U8, name="x_sc", align_bytes=64)
-        nc.vector.tensor_copy(x_sc[:], scale_table[:].indirect(offs_sb[:]))
-        x_codes = keep.tile([P, S], U32, name="x_codes", align_bytes=64)
-        nc.vector.tensor_copy(x_codes[:], x_table[:].indirect(offs_sb[:]))
 
         w1_bf = [keep.tile([P, 2, P, PACK], BF16, name="w1_bf%d" % u, align_bytes=64) for u in range(2)]
         w1_codes = [keep.tile([P, 2 * P], U32, name="w1_codes%d" % u, align_bytes=64) for u in range(2)]
         w1_sc = [keep.tile([P, 2 * P], U8, name="w1_sc%d" % u, align_bytes=64) for u in range(2)]
-
-        def cast_w1(i, u):
-            c0, n = W1_PIECES[i]
-            dst = w1_bf[u][:, :, c0 // PACK : (c0 + n) // PACK, :].rearrange("p e m j -> p m j e")
-            src = w1_raw[i][:].rearrange("p j (m t) -> p m j t", t=PACK)[:, :, :, 2 * u : 2 * u + 2]
-            if i < 2:
-                nc.scalar.copy(dst, src)
-            else:
-                nc.vector.tensor_copy(dst, src)
-
-        def quantize_w1(u, e0, e1):
-            cols = slice(P * e0, P * e1)
-            nc.vector.quantize_mx(
-                out=w1_codes[u][:, cols].bitcast(FP8X4),
-                scales=w1_sc[u][:, cols],
-                in_=w1_bf[u][:, e0:e1, :, :].rearrange("p e m j -> p (e m j)"),
-            )
-
+        w1_cols = w1_raw[:].rearrange("p j (m t) -> p m j t", t=PACK)
+        nc.vector.tensor_copy(w1_bf[0][:].rearrange("p e m j -> p m j e"), w1_cols[:, :, :, 0:2])
+        nc.scalar.copy(w1_bf[1][:].rearrange("p e m j -> p m j e"), w1_cols[:, :, :, 2:4])
+        x_sc = keep.tile([P, S], U8, name="x_sc", align_bytes=64)
+        nc.vector.tensor_copy(x_sc[:], scale_table[:].indirect(offs_sb[:]))
         for u in range(2):
-            for i in range(len(W1_PIECES)):
-                cast_w1(i, u)
-            if u == 0:
-                quantize_w1(0, 0, 1)
-        quantize_w1(0, 1, 2)
-        quantize_w1(1, 0, 2)
+            nc.vector.quantize_mx(out=w1_codes[u][:].bitcast(FP8X4), scales=w1_sc[u][:], in_=w1_bf[u][:].rearrange("p e m j -> p (e m j)"))
 
-        up_sb = keep.tile([P, PACK, S], F32, name="up_sb", tag="raw0")
-        nc.sync.dma_start(up_sb[:], up.rearrange("(p t) s -> p t s", t=PACK))
-        w2_raw = keep.tile([P, PACK, N], F32, name="w2_raw", tag="raw1")
-        nc.sync.dma_start(w2_raw[:], w2.rearrange("(p t) n -> p t n", t=PACK))
+        late = keep.tile([P, 2 * PACK, H], F32, name="late", tag="raw")
+        up_sb = late[:, 0:PACK, :]
+        w2_raw = late[:, PACK : 2 * PACK, :]
+        nc.sync.dma_start(up_sb, up.rearrange("(p t) s -> p t s", t=PACK))
+        nc.sync.dma_start(w2_raw, w2.rearrange("(p t) n -> p t n", t=PACK))
 
-        halves = [slice(0, HALF), slice(HALF, S)]
+        x_codes = keep.tile([P, S], U32, name="x_codes", align_bytes=64)
+        for h in range(2):
+            nc.vector.tensor_copy(x_codes[:, halves[h]], x_table[:].indirect(offs_sb[:, 16 * h : 16 * h + 16]))
+
         y_plain = keep.tile([P, PACK, S], F32, name="y_plain")
         diff = keep.tile([P, PACK, S], F32, name="diff")
-        banks = 0
+        y_banks = []
         for t in range(PACK):
             cols = slice(P * (t % 2), P * (t % 2) + P)
-            window = keep.tile([P, S if t == 0 else 2 * S], F32, name="y_window%d" % t)
-            if t > 0:
-                nc.gpsimd.memset(window[:, S : 2 * S], 0.0)
+            window = keep.tile([P, S], F32, name="y_window", tag="window%d" % t)
             for piece in halves if t == 0 else [slice(0, S)]:
                 n = piece.stop - piece.start
-                bank = psum.tile([P, n], F32, name="y_bank", tag="bank%d" % banks)
-                banks = banks + 1
+                bank = psum.tile([P, n], F32, name="y_bank", tag="bank%d" % len(y_banks))
+                y_banks.append((t, piece, bank))
                 nc.tensor.matmul_mx(
                     out=bank[:],
                     lhsT=w1_codes[t // 2][:, cols].bitcast(FP8X4),
@@ -113,50 +86,49 @@ def tile_picked_cmpex_none_p_kernel(tc, x_words, x_scales, w1, up, w2, offs, mat
                 else:
                     nc.scalar.copy(window[:, piece], bank[:])
                 nc.scalar.copy(y_plain[:, t, piece], bank[:])
-            for piece in halves if t == 0 else [slice(0, S)]:
-                picks = mate_sb[:, piece.start // 16 : piece.stop // 16]
-                nc.vector.tensor_tensor(diff[:, t, piece], window[:].indirect(picks), y_plain[:, t, piece], ALU.subtract)
+            for h in range(2):
+                nc.vector.tensor_tensor(diff[:, t, halves[h]], window[:].indirect(mate_sb[:, 16 * h : 16 * h + 16]), y_plain[:, t, halves[h]], ALU.subtract)
 
         gaps = []
-        for h in range(2):
-            gap = keep.tile([P, PACK, HALF], F32, name="gap%d" % h)
-            nc.scalar.activation(gap[:], diff[:, :, halves[h]], ACT.Abs)
+        for u in range(2):
+            gap = keep.tile([P, 2, S], F32, name="gap%d" % u)
+            nc.scalar.activation(gap[:], diff[:, 2 * u : 2 * u + 2, :], ACT.Abs)
             gaps.append(gap)
 
         w2_bf = keep.tile([P, N, PACK], BF16, name="w2_bf", align_bytes=64)
         for h in range(2):
-            ns = slice(HALF * h, HALF * h + HALF)
             nc.scalar.copy(
-                w2_bf[:, ns, :].rearrange("p (c i) t -> p c t i", i=2),
-                w2_raw[:, :, ns].rearrange("p t (c i) -> p c t i", i=2),
+                w2_bf[:, halves[h], :].rearrange("p (c i) t -> p c t i", i=2),
+                w2_raw[:, :, halves[h]].rearrange("p t (c i) -> p c t i", i=2),
             )
         w2_codes = keep.tile([P, N], U32, name="w2_codes", align_bytes=64)
         w2_sc = keep.tile([P, N], U8, name="w2_sc", align_bytes=64)
 
-        def lower(h):
-            lo = keep.tile([P, PACK, HALF], F32, name="lo%d" % h)
-            nc.vector.scalar_tensor_tensor(lo[:], diff[:, :, halves[h]], 0.0, y_plain[:, :, halves[h]], ALU.min, ALU.add)
-            return lo
+        part = keep.tile([P, PACK, S], F32, name="part")
+        nc.gpsimd.tensor_tensor(part[:, 0:2, :], gaps[0][:], up_sb[:, 0:2, :], ALU.mult)
 
-        def share(h):
-            part = keep.tile([P, PACK, HALF], F32, name="part%d" % h)
-            nc.vector.tensor_tensor(part[:], gaps[h][:], up_sb[:, :, halves[h]], ALU.mult)
-            return part
+        lo = keep.tile([P, PACK, S], F32, name="lo", tag="window%d" % (PACK - 1))
+        for t, piece, bank in y_banks:
+            nc.vector.scalar_tensor_tensor(lo[:, t, piece], diff[:, t, piece], 0.0, bank[:], ALU.min, ALU.add)
 
-        def mix(c, lo, part):
+        def share(c):
             c0, n = CHUNKS[c]
-            cols = slice(c0 % HALF, c0 % HALF + n)
+            nc.vector.tensor_tensor(part[:, 2:4, c0 : c0 + n], gaps[1][:, :, c0 : c0 + n], up_sb[:, 2:4, c0 : c0 + n], ALU.mult)
+
+        def mix(c):
+            c0, n = CHUNKS[c]
             z_bf = keep.tile([P, n, PACK], BF16, name="z_bf%d" % c, align_bytes=64)
             nc.vector.tensor_tensor(
                 z_bf[:].rearrange("p (c i) t -> p c t i", i=2),
-                lo[:, :, cols].rearrange("p t (c i) -> p c t i", i=2),
-                part[:, :, cols].rearrange("p t (c i) -> p c t i", i=2),
+                lo[:, :, c0 : c0 + n].rearrange("p t (c i) -> p c t i", i=2),
+                part[:, :, c0 : c0 + n].rearrange("p t (c i) -> p c t i", i=2),
                 ALU.add,
             )
             return z_bf
 
         def finish(c, z_bf, bank0):
             c0, n = CHUNKS[c]
+            last = c == len(CHUNKS) - 1
             codes = keep.tile([P, n], U32, name="z_codes%d" % c, align_bytes=64)
             sc = keep.tile([P, n], U8, name="z_sc%d" % c, align_bytes=64)
             nc.vector.quantize_mx(out=codes[:].bitcast(FP8X4), scales=sc[:], in_=z_bf[:].rearrange("p n t -> p (n t)"))
@@ -174,21 +146,20 @@ def tile_picked_cmpex_none_p_kernel(tc, x_words, x_scales, w1, up, w2, offs, mat
                         stop=True,
                     )
                 res = keep.tile([P, 2, n], F32, name="res%d_%d" % (c, b))
-                if c == len(CHUNKS) - 1 and b == 1:
+                if last and b == 1:
                     nc.vector.tensor_copy(res[:], bank[:])
                 else:
                     nc.scalar.copy(res[:], bank[:])
-                queue = nc.scalar if c == len(CHUNKS) - 1 and b == 0 else nc.sync
+                queue = nc.scalar if last and b == 0 else nc.sync
                 queue.dma_start(out[2 * P * b : 2 * P * (b + 1), c0 : c0 + n].rearrange("(e p) s -> p e s", p=P), res[:])
 
-        lo0 = lower(0)
-        part0 = share(0)
-        lo1 = lower(1)
-        z0 = mix(0, lo0, part0)
-        part1 = share(1)
+        share(0)
+        share(1)
+        z0 = mix(0)
         nc.vector.quantize_mx(out=w2_codes[:].bitcast(FP8X4), scales=w2_sc[:], in_=w2_bf[:].rearrange("p n t -> p (n t)"))
         finish(0, z0, 0)
-        z1 = mix(1, lo1, part1)
-        z2 = mix(2, lo1, part1)
+        z1 = mix(1)
+        share(2)
         finish(1, z1, 2)
+        z2 = mix(2)
         finish(2, z2, 4)

@@ -62,13 +62,15 @@ def tile_picked_cmpex_none_p_kernel(tc, x_words, x_scales, w1, up, w2, offs, mat
         for h in range(2):
             nc.vector.tensor_copy(x_codes[:, halves[h]], x_table[:].indirect(offs_sb[:, 16 * h : 16 * h + 16]))
 
-        y_plain = keep.tile([P, PACK, S], F32, name="y_plain")
         diff = keep.tile([P, PACK, S], F32, name="diff")
+        tables = [keep.tile([P, S if t == 0 else 2 * S], F32, name="y_table%d" % t, tag="table%d" % t) for t in range(PACK)]
+        last_plain = keep.tile([P, S], F32, name="last_plain")
         y_banks = []
         for t in range(PACK):
             cols = slice(P * (t % 2), P * (t % 2) + P)
-            window = keep.tile([P, S], F32, name="y_window", tag="window%d" % t)
-            for piece in halves if t == 0 else [slice(0, S)]:
+            plain = tables[t + 1][:, S : 2 * S] if t + 1 < PACK else last_plain[:]
+            pieces = halves if t == 0 else [slice(0, S)]
+            for piece in pieces:
                 n = piece.stop - piece.start
                 bank = psum.tile([P, n], F32, name="y_bank", tag="bank%d" % len(y_banks))
                 y_banks.append((t, piece, bank))
@@ -82,32 +84,31 @@ def tile_picked_cmpex_none_p_kernel(tc, x_words, x_scales, w1, up, w2, offs, mat
                     stop=True,
                 )
                 if t == 0 and piece.start > 0:
-                    nc.vector.tensor_copy(window[:, piece], bank[:])
+                    nc.vector.tensor_copy(tables[t][:, piece], bank[:])
                 else:
-                    nc.scalar.copy(window[:, piece], bank[:])
-                nc.scalar.copy(y_plain[:, t, piece], bank[:])
-            for h in range(2):
-                nc.vector.tensor_tensor(diff[:, t, halves[h]], window[:].indirect(mate_sb[:, 16 * h : 16 * h + 16]), y_plain[:, t, halves[h]], ALU.subtract)
+                    nc.scalar.copy(tables[t][:, piece], bank[:])
+                nc.scalar.copy(plain[:, piece], bank[:])
+            for piece in pieces:
+                mates = mate_sb[:, piece.start // 16 : piece.stop // 16]
+                nc.vector.tensor_tensor(diff[:, t, piece], tables[t][:].indirect(mates), plain[:, piece], ALU.subtract)
 
         gaps = []
+        w2_bf = keep.tile([P, N, PACK], BF16, name="w2_bf", align_bytes=64)
         for u in range(2):
             gap = keep.tile([P, 2, S], F32, name="gap%d" % u)
             nc.scalar.activation(gap[:], diff[:, 2 * u : 2 * u + 2, :], ACT.Abs)
             gaps.append(gap)
-
-        w2_bf = keep.tile([P, N, PACK], BF16, name="w2_bf", align_bytes=64)
-        for h in range(2):
             nc.scalar.copy(
-                w2_bf[:, halves[h], :].rearrange("p (c i) t -> p c t i", i=2),
-                w2_raw[:, :, halves[h]].rearrange("p t (c i) -> p c t i", i=2),
+                w2_bf[:, halves[u], :].rearrange("p (c i) t -> p c t i", i=2),
+                w2_raw[:, :, halves[u]].rearrange("p t (c i) -> p c t i", i=2),
             )
         w2_codes = keep.tile([P, N], U32, name="w2_codes", align_bytes=64)
         w2_sc = keep.tile([P, N], U8, name="w2_sc", align_bytes=64)
 
-        part = keep.tile([P, PACK, S], F32, name="part")
+        part = keep.tile([P, PACK, S], F32, name="part", tag="table%d" % (PACK - 2))
         nc.gpsimd.tensor_tensor(part[:, 0:2, :], gaps[0][:], up_sb[:, 0:2, :], ALU.mult)
 
-        lo = keep.tile([P, PACK, S], F32, name="lo", tag="window%d" % (PACK - 1))
+        lo = keep.tile([P, PACK, S], F32, name="lo", tag="table%d" % (PACK - 1))
         for t, piece, bank in y_banks:
             nc.vector.scalar_tensor_tensor(lo[:, t, piece], diff[:, t, piece], 0.0, bank[:], ALU.min, ALU.add)
 

@@ -64,16 +64,18 @@ def tile_picked_cmpex_none_p_kernel(tc, x_words, x_scales, w1, up, w2, offs, mat
 
         diff = keep.tile([P, PACK, S], F32, name="diff")
         tables = [keep.tile([P, S if t == 0 else 2 * S], F32, name="y_table%d" % t, tag="table%d" % t) for t in range(PACK)]
-        last_plain = keep.tile([P, S], F32, name="last_plain")
+        last_plain = keep.tile([P, S], F32, name="last_plain", tag="last_plain", align_bytes=64)
         y_banks = []
         for t in range(PACK):
             cols = slice(P * (t % 2), P * (t % 2) + P)
             plain = tables[t + 1][:, S : 2 * S] if t + 1 < PACK else last_plain[:]
-            pieces = halves if t == 0 else [slice(0, S)]
+            pieces = [slice(0, HALF), slice(HALF, HALF + P), slice(HALF + P, S)] if t == 0 else [slice(0, S)]
+            made = []
             for piece in pieces:
                 n = piece.stop - piece.start
                 bank = psum.tile([P, n], F32, name="y_bank", tag="bank%d" % len(y_banks))
                 y_banks.append((t, piece, bank))
+                made.append((piece, bank))
                 nc.tensor.matmul_mx(
                     out=bank[:],
                     lhsT=w1_codes[t // 2][:, cols].bitcast(FP8X4),
@@ -83,21 +85,21 @@ def tile_picked_cmpex_none_p_kernel(tc, x_words, x_scales, w1, up, w2, offs, mat
                     start=True,
                     stop=True,
                 )
-                if t == 0 and piece.start > 0:
-                    nc.vector.tensor_copy(tables[t][:, piece], bank[:])
+                nc.scalar.copy(tables[t][:, piece], bank[:])
+            for piece, bank in made:
+                if t == 0 and piece.start == 0:
+                    nc.vector.tensor_copy(plain[:, piece], bank[:])
                 else:
-                    nc.scalar.copy(tables[t][:, piece], bank[:])
-                nc.scalar.copy(plain[:, piece], bank[:])
-            for piece in pieces:
+                    nc.scalar.copy(plain[:, piece], bank[:])
+            for piece in halves if t == 0 else pieces:
                 mates = mate_sb[:, piece.start // 16 : piece.stop // 16]
                 nc.vector.tensor_tensor(diff[:, t, piece], tables[t][:].indirect(mates), plain[:, piece], ALU.subtract)
 
-        gaps = []
-        w2_bf = keep.tile([P, N, PACK], BF16, name="w2_bf", align_bytes=64)
+        gap = keep.tile([P, PACK, S], F32, name="gap")
+        for t in range(PACK):
+            nc.scalar.activation(gap[:, t, :], diff[:, t, :], ACT.Abs)
+        w2_bf = keep.tile([P, N, PACK], BF16, name="w2_bf", tag="last_plain", align_bytes=64)
         for u in range(2):
-            gap = keep.tile([P, 2, S], F32, name="gap%d" % u)
-            nc.scalar.activation(gap[:], diff[:, 2 * u : 2 * u + 2, :], ACT.Abs)
-            gaps.append(gap)
             nc.scalar.copy(
                 w2_bf[:, halves[u], :].rearrange("p (c i) t -> p c t i", i=2),
                 w2_raw[:, :, halves[u]].rearrange("p t (c i) -> p c t i", i=2),
@@ -106,7 +108,8 @@ def tile_picked_cmpex_none_p_kernel(tc, x_words, x_scales, w1, up, w2, offs, mat
         w2_sc = keep.tile([P, N], U8, name="w2_sc", align_bytes=64)
 
         part = keep.tile([P, PACK, S], F32, name="part", tag="table%d" % (PACK - 2))
-        nc.gpsimd.tensor_tensor(part[:, 0:2, :], gaps[0][:], up_sb[:, 0:2, :], ALU.mult)
+        for t in range(2):
+            nc.gpsimd.tensor_tensor(part[:, t, :], gap[:, t, :], up_sb[:, t, :], ALU.mult)
 
         lo = keep.tile([P, PACK, S], F32, name="lo", tag="table%d" % (PACK - 1))
         for t, piece, bank in y_banks:
@@ -114,7 +117,7 @@ def tile_picked_cmpex_none_p_kernel(tc, x_words, x_scales, w1, up, w2, offs, mat
 
         def share(c):
             c0, n = CHUNKS[c]
-            nc.vector.tensor_tensor(part[:, 2:4, c0 : c0 + n], gaps[1][:, :, c0 : c0 + n], up_sb[:, 2:4, c0 : c0 + n], ALU.mult)
+            nc.vector.tensor_tensor(part[:, 2:4, c0 : c0 + n], gap[:, 2:4, c0 : c0 + n], up_sb[:, 2:4, c0 : c0 + n], ALU.mult)
 
         def mix(c):
             c0, n = CHUNKS[c]

@@ -65,35 +65,47 @@ def tile_picked_cmpex_none_p_kernel(tc, x_words, x_scales, w1, up, w2, offs, mat
         diff = keep.tile([P, PACK, S], F32, name="diff")
         tables = [keep.tile([P, S if t == 0 else 2 * S], F32, name="y_table%d" % t, tag="table%d" % t) for t in range(PACK)]
         last_plain = keep.tile([P, S], F32, name="last_plain", tag="last_plain", align_bytes=64)
+        plains = [tables[t + 1][:, S : 2 * S] if t + 1 < PACK else last_plain[:] for t in range(PACK)]
         y_banks = []
-        for t in range(PACK):
+
+        def product(t, piece):
             cols = slice(P * (t % 2), P * (t % 2) + P)
-            plain = tables[t + 1][:, S : 2 * S] if t + 1 < PACK else last_plain[:]
-            pieces = [slice(0, HALF), slice(HALF, HALF + P), slice(HALF + P, S)] if t == 0 else [slice(0, S)]
-            made = []
-            for piece in pieces:
-                n = piece.stop - piece.start
-                bank = psum.tile([P, n], F32, name="y_bank", tag="bank%d" % len(y_banks))
-                y_banks.append((t, piece, bank))
-                made.append((piece, bank))
-                nc.tensor.matmul_mx(
-                    out=bank[:],
-                    lhsT=w1_codes[t // 2][:, cols].bitcast(FP8X4),
-                    lhsT_scale=w1_sc[t // 2][:, cols],
-                    rhs=x_codes[:, piece].bitcast(FP8X4),
-                    rhs_scale=x_sc[:, piece],
-                    start=True,
-                    stop=True,
-                )
-                nc.scalar.copy(tables[t][:, piece], bank[:])
-            for piece, bank in made:
-                if t == 0 and piece.start == 0:
-                    nc.vector.tensor_copy(plain[:, piece], bank[:])
-                else:
-                    nc.scalar.copy(plain[:, piece], bank[:])
-            for piece in halves if t == 0 else pieces:
-                mates = mate_sb[:, piece.start // 16 : piece.stop // 16]
-                nc.vector.tensor_tensor(diff[:, t, piece], tables[t][:].indirect(mates), plain[:, piece], ALU.subtract)
+            bank = psum.tile([P, piece.stop - piece.start], F32, name="y_bank", tag="bank%d" % len(y_banks))
+            y_banks.append((t, piece, bank))
+            nc.tensor.matmul_mx(
+                out=bank[:],
+                lhsT=w1_codes[t // 2][:, cols].bitcast(FP8X4),
+                lhsT_scale=w1_sc[t // 2][:, cols],
+                rhs=x_codes[:, piece].bitcast(FP8X4),
+                rhs_scale=x_sc[:, piece],
+                start=True,
+                stop=True,
+            )
+            return bank
+
+        def fetch(t, piece):
+            mates = mate_sb[:, piece.start // 16 : piece.stop // 16]
+            nc.vector.tensor_tensor(diff[:, t, piece], tables[t][:].indirect(mates), plains[t][:, piece], ALU.subtract)
+
+        early = [product(t, halves[0]) for t in range(2)]
+        nc.scalar.copy(tables[0][:, halves[0]], early[0][:])
+        quarters = [slice(HALF, HALF + P), slice(HALF + P, S)]
+        rest = [product(0, piece) for piece in quarters]
+        for piece, bank in zip(quarters, rest):
+            nc.scalar.copy(tables[0][:, piece], bank[:])
+        for t in range(2):
+            nc.vector.tensor_copy(plains[t][:, halves[0]], early[t][:])
+        for piece, bank in zip(quarters, rest):
+            nc.scalar.copy(plains[0][:, piece], bank[:])
+        for piece in halves:
+            fetch(0, piece)
+        nc.scalar.copy(tables[1][:, halves[0]], early[1][:])
+        for t in range(1, PACK):
+            piece = halves[1] if t == 1 else slice(0, S)
+            bank = product(t, piece)
+            nc.scalar.copy(tables[t][:, piece], bank[:])
+            nc.scalar.copy(plains[t][:, piece], bank[:])
+            fetch(t, slice(0, S))
 
         gap = keep.tile([P, PACK, S], F32, name="gap")
         for t in range(PACK):
@@ -136,10 +148,11 @@ def tile_picked_cmpex_none_p_kernel(tc, x_words, x_scales, w1, up, w2, offs, mat
             codes = keep.tile([P, n], U32, name="z_codes%d" % c, align_bytes=64)
             sc = keep.tile([P, n], U8, name="z_sc%d" % c, align_bytes=64)
             nc.vector.quantize_mx(out=codes[:].bitcast(FP8X4), scales=sc[:], in_=z_bf[:].rearrange("p n t -> p (n t)"))
-            for b in range(2):
-                bank = psum.tile([P, 2, n], F32, name="o_bank", tag="bank%d" % (bank0 + b))
-                for e in range(2):
-                    cols = slice(P * (2 * b + e), P * (2 * b + e) + P)
+            rows = 1 if last else 2
+            for b in range(PACK // rows):
+                bank = psum.tile([P, rows, n], F32, name="o_bank", tag="bank%d" % (bank0 + b))
+                for e in range(rows):
+                    cols = slice(P * (rows * b + e), P * (rows * b + e) + P)
                     nc.tensor.matmul_mx(
                         out=bank[:, e, :],
                         lhsT=w2_codes[:, cols].bitcast(FP8X4),
@@ -149,13 +162,14 @@ def tile_picked_cmpex_none_p_kernel(tc, x_words, x_scales, w1, up, w2, offs, mat
                         start=True,
                         stop=True,
                     )
-                res = keep.tile([P, 2, n], F32, name="res%d_%d" % (c, b))
-                if last and b == 1:
+                res = keep.tile([P, rows, n], F32, name="res%d_%d" % (c, b))
+                by_vector = last and b % 2 == 1
+                if by_vector:
                     nc.vector.tensor_copy(res[:], bank[:])
                 else:
                     nc.scalar.copy(res[:], bank[:])
-                queue = nc.scalar if last and b == 0 else nc.sync
-                queue.dma_start(out[2 * P * b : 2 * P * (b + 1), c0 : c0 + n].rearrange("(e p) s -> p e s", p=P), res[:])
+                queue = nc.scalar if last and b >= 2 else nc.sync
+                queue.dma_start(out[rows * P * b : rows * P * (b + 1), c0 : c0 + n].rearrange("(e p) s -> p e s", p=P), res[:])
 
         share(0)
         share(1)

@@ -45,11 +45,12 @@ def tile_picked_cmpex_none_p_kernel(tc, x_words, x_scales, w1, up, w2, offs, mat
         w1_codes = [keep.tile([P, 2 * P], U32, name="w1_codes%d" % u, align_bytes=64) for u in range(2)]
         w1_sc = [keep.tile([P, 2 * P], U8, name="w1_sc%d" % u, align_bytes=64) for u in range(2)]
         w1_cols = w1_raw[:].rearrange("p j (m t) -> p m j t", t=PACK)
-        nc.vector.tensor_copy(w1_bf[0][:].rearrange("p e m j -> p m j e"), w1_cols[:, :, :, 0:2])
+        nc.vector.tensor_copy(w1_bf[0][:, :, 0 : P // 2, :].rearrange("p e m j -> p m j e"), w1_cols[:, 0 : P // 2, :, 0:2])
         nc.scalar.copy(w1_bf[1][:].rearrange("p e m j -> p m j e"), w1_cols[:, :, :, 2:4])
+        nc.scalar.copy(w1_bf[0][:, :, P // 2 : P, :].rearrange("p e m j -> p m j e"), w1_cols[:, P // 2 : P, :, 0:2])
         x_sc = keep.tile([P, S], U8, name="x_sc", align_bytes=64)
         nc.vector.tensor_copy(x_sc[:], scale_table[:].indirect(offs_sb[:]))
-        for u in range(2):
+        for u in (1, 0):
             nc.vector.quantize_mx(out=w1_codes[u][:].bitcast(FP8X4), scales=w1_sc[u][:], in_=w1_bf[u][:].rearrange("p e m j -> p (e m j)"))
 
         late = keep.tile([P, 2 * PACK, H], F32, name="late", tag="raw")

@@ -1,6 +1,7 @@
 from contextlib import ExitStack
 
 import concourse.mybir as mybir
+from concourse.masks import make_identity
 
 K, T, S, N, H = 512, 2048, 512, 512, 512
 FLOPS = 2 * K * H * S + 2 * H * N * S
@@ -18,7 +19,6 @@ ACT = mybir.ActivationFunctionType
 P = 128
 PACK = 4
 HALF = S // 2
-CHUNKS = [(0, 256), (256, 128), (384, 128)]
 
 
 def tile_picked_cmpex_none_p_kernel(tc, x_words, x_scales, w1, up, w2, offs, mate, out):
@@ -63,7 +63,9 @@ def tile_picked_cmpex_none_p_kernel(tc, x_words, x_scales, w1, up, w2, offs, mat
         for h in range(2):
             nc.vector.tensor_copy(x_codes[:, halves[h]], x_table[:].indirect(offs_sb[:, 16 * h : 16 * h + 16]))
 
-        diff = keep.tile([P, PACK, S], F32, name="diff")
+        ident = keep.tile([P, P], F32, name="ident")
+        make_identity(nc, ident[:])
+        diffs = [keep.tile([P, 2, S], F32, name="diff%d" % u, tag="diff%d" % u, align_bytes=64) for u in range(2)]
         tables = [keep.tile([P, S if t == 0 else 2 * S], F32, name="y_table%d" % t, tag="table%d" % t) for t in range(PACK)]
         last_plain = keep.tile([P, S], F32, name="last_plain", tag="last_plain", align_bytes=64)
         plains = [tables[t + 1][:, S : 2 * S] if t + 1 < PACK else last_plain[:] for t in range(PACK)]
@@ -86,7 +88,7 @@ def tile_picked_cmpex_none_p_kernel(tc, x_words, x_scales, w1, up, w2, offs, mat
 
         def fetch(t, piece):
             mates = mate_sb[:, piece.start // 16 : piece.stop // 16]
-            nc.vector.tensor_tensor(diff[:, t, piece], tables[t][:].indirect(mates), plains[t][:, piece], ALU.subtract)
+            nc.vector.tensor_tensor(diffs[t // 2][:, t % 2, piece], tables[t][:].indirect(mates), plains[t][:, piece], ALU.subtract)
 
         early = [product(t, halves[0]) for t in range(2)]
         nc.scalar.copy(tables[0][:, halves[0]], early[0][:])
@@ -108,50 +110,96 @@ def tile_picked_cmpex_none_p_kernel(tc, x_words, x_scales, w1, up, w2, offs, mat
             nc.scalar.copy(plains[t][:, piece], bank[:])
             fetch(t, slice(0, S))
 
-        gap = keep.tile([P, PACK, S], F32, name="gap")
+        first, second = halves
+        sums = [psum.tile([P, PACK, P], F32, name="sum_bank", tag="bank%d" % c) for c in range(2)]
+
+        def add_turned(c, t, source, start=False, stop=False):
+            nc.tensor.matmul(sums[c][:, t, :], source[:, P * c : P * c + P], ident[:], is_transpose=True, start=start, stop=stop)
+
         for t in range(PACK):
-            nc.scalar.activation(gap[:, t, :], diff[:, t, :], ACT.Abs)
-        w2_bf = keep.tile([P, N, PACK], BF16, name="w2_bf", tag="last_plain", align_bytes=64)
-        for u in range(2):
-            nc.scalar.copy(
-                w2_bf[:, halves[u], :].rearrange("p (c i) t -> p c t i", i=2),
+            for c in range(2):
+                add_turned(c, t, tables[t][:, 0:S], start=t == 0)
+                add_turned(c, t, plains[t])
+                add_turned(c, t, diffs[t // 2][:, t % 2, :])
+
+        gap1 = keep.tile([P, PACK, HALF], F32, name="gap1", tag="gap1")
+        gap2 = keep.tile([P, PACK, HALF], F32, name="gap2")
+        slope = keep.tile([P, PACK, HALF], F32, name="slope")
+        nc.scalar.activation(gap1[:, 0:2, :], diffs[0][:, :, first], ACT.Abs, scale=2.0)
+        nc.scalar.activation(gap1[:, 2, :], diffs[1][:, 0, first], ACT.Abs, scale=2.0)
+        nc.scalar.activation(gap2[:, 0:2, :], diffs[0][:, :, second], ACT.Abs)
+        nc.scalar.activation(gap1[:, 3, :], diffs[1][:, 1, first], ACT.Abs, scale=2.0)
+        nc.scalar.activation(gap2[:, 2:4, :], diffs[1][:, :, second], ACT.Abs)
+        for planes in (slice(0, 3), slice(3, 4)):
+            nc.vector.scalar_tensor_tensor(slope[:, planes, :], up_sb[:, planes, first], 0.5, gap1[:, planes, :], ALU.subtract, ALU.mult)
+        for t in range(PACK):
+            for c in range(2):
+                add_turned(c, t, slope[:, t, :], stop=t == PACK - 1)
+
+        part = up_sb[:, :, first]
+        nc.gpsimd.tensor_tensor(part[:, 2:4, :], gap2[:, 2:4, :], up_sb[:, 2:4, second], ALU.mult)
+        lo = keep.tile([P, PACK, HALF], F32, name="lo", tag="gap1")
+        for t, piece, bank in y_banks:
+            if piece.stop > HALF:
+                c0 = max(piece.start, HALF)
+                nc.vector.scalar_tensor_tensor(
+                    lo[:, t, c0 - HALF : piece.stop - HALF], diffs[t // 2][:, t % 2, c0 : piece.stop], 0.0, bank[:, c0 - piece.start :], ALU.min, ALU.add
+                )
+
+        w2_bf = [
+            keep.tile([P, HALF, PACK], BF16, name="w2_bf%d" % u, tag=tag, align_bytes=64) for u, tag in enumerate(("last_plain", "diff0"))
+        ]
+        for u, copy in enumerate((nc.scalar.copy, nc.vector.tensor_copy)):
+            copy(
+                w2_bf[u][:].rearrange("p (c i) t -> p c t i", i=2),
                 w2_raw[:, :, halves[u]].rearrange("p t (c i) -> p c t i", i=2),
             )
-        w2_codes = keep.tile([P, N], U32, name="w2_codes", align_bytes=64)
+        w2_codes = keep.tile([P, N], U32, name="w2_codes", tag="diff1", align_bytes=64)
         w2_sc = keep.tile([P, N], U8, name="w2_sc", align_bytes=64)
+        for u in range(2):
+            nc.vector.quantize_mx(out=w2_codes[:, halves[u]].bitcast(FP8X4), scales=w2_sc[:, halves[u]], in_=w2_bf[u][:].rearrange("p n t -> p (n t)"))
 
-        part = keep.tile([P, PACK, S], F32, name="part", tag="table%d" % (PACK - 2))
-        for t in range(2):
-            nc.gpsimd.tensor_tensor(part[:, t, :], gap[:, t, :], up_sb[:, t, :], ALU.mult)
-
-        lo = keep.tile([P, PACK, S], F32, name="lo", tag="table%d" % (PACK - 1))
-        for t, piece, bank in y_banks:
-            nc.vector.scalar_tensor_tensor(lo[:, t, piece], diff[:, t, piece], 0.0, bank[:], ALU.min, ALU.add)
+        backs = []
+        for c, tag in enumerate(("bank7", "bank2")):
+            turned = keep.tile([P, 2, P, 2], BF16, name="turned%d" % c)
+            nc.scalar.activation(turned[:], sums[c][:].rearrange("j (u e) p -> j u p e", e=2), ACT.Copy, scale=0.5)
+            words = turned[:].rearrange("j u p e -> j u (p e)").bitcast(F32)
+            back = psum.tile([P, 2, P], F32, name="back_bank", tag=tag)
+            for u in range(2):
+                nc.tensor.transpose(back[:, u, :], words[:, u, :], ident[:])
+            backs.append(back)
+        z_first = []
+        for c in range(2):
+            z_bf = keep.tile([P, P, PACK], BF16, name="z_first%d" % c, align_bytes=64)
+            nc.scalar.copy(
+                z_bf[:].rearrange("p n t -> p (n t)").bitcast(F32).rearrange("p (j u) -> p j u", u=2),
+                backs[c][:].rearrange("p u j -> p j u"),
+            )
+            z_first.append(z_bf)
 
         def share(c):
-            c0, n = CHUNKS[c]
-            nc.vector.tensor_tensor(part[:, 2:4, c0 : c0 + n], gap[:, 2:4, c0 : c0 + n], up_sb[:, 2:4, c0 : c0 + n], ALU.mult)
+            cols = slice(P * c, P * c + P)
+            nc.vector.tensor_tensor(part[:, 0:2, cols], gap2[:, 0:2, cols], up_sb[:, 0:2, HALF + P * c : HALF + P * c + P], ALU.mult)
 
         def mix(c):
-            c0, n = CHUNKS[c]
-            z_bf = keep.tile([P, n, PACK], BF16, name="z_bf%d" % c, align_bytes=64)
+            cols = slice(P * c, P * c + P)
+            z_bf = keep.tile([P, P, PACK], BF16, name="z_bf%d" % c, align_bytes=64)
             nc.vector.tensor_tensor(
                 z_bf[:].rearrange("p (c i) t -> p c t i", i=2),
-                lo[:, :, c0 : c0 + n].rearrange("p t (c i) -> p c t i", i=2),
-                part[:, :, c0 : c0 + n].rearrange("p t (c i) -> p c t i", i=2),
+                lo[:, :, cols].rearrange("p t (c i) -> p c t i", i=2),
+                part[:, :, cols].rearrange("p t (c i) -> p c t i", i=2),
                 ALU.add,
             )
             return z_bf
 
-        def finish(c, z_bf, bank0):
-            c0, n = CHUNKS[c]
-            last = c == len(CHUNKS) - 1
-            codes = keep.tile([P, n], U32, name="z_codes%d" % c, align_bytes=64)
-            sc = keep.tile([P, n], U8, name="z_sc%d" % c, align_bytes=64)
+        def finish(c0, n, z_bf, banks):
+            last = c0 + n == S
+            codes = keep.tile([P, n], U32, name="z_codes%d" % c0, align_bytes=64)
+            sc = keep.tile([P, n], U8, name="z_sc%d" % c0, align_bytes=64)
             nc.vector.quantize_mx(out=codes[:].bitcast(FP8X4), scales=sc[:], in_=z_bf[:].rearrange("p n t -> p (n t)"))
             rows = 1 if last else 2
             for b in range(PACK // rows):
-                bank = psum.tile([P, rows, n], F32, name="o_bank", tag="bank%d" % (bank0 + b))
+                bank = psum.tile([P, rows, n], F32, name="o_bank", tag="bank%d" % banks[b])
                 for e in range(rows):
                     cols = slice(P * (rows * b + e), P * (rows * b + e) + P)
                     nc.tensor.matmul_mx(
@@ -163,7 +211,7 @@ def tile_picked_cmpex_none_p_kernel(tc, x_words, x_scales, w1, up, w2, offs, mat
                         start=True,
                         stop=True,
                     )
-                res = keep.tile([P, rows, n], F32, name="res%d_%d" % (c, b))
+                res = keep.tile([P, rows, n], F32, name="res%d_%d" % (c0, b))
                 by_vector = last and b % 2 == 1
                 if by_vector:
                     nc.vector.tensor_copy(res[:], bank[:])
@@ -173,12 +221,10 @@ def tile_picked_cmpex_none_p_kernel(tc, x_words, x_scales, w1, up, w2, offs, mat
                 queue.dma_start(out[rows * P * b : rows * P * (b + 1), c0 : c0 + n].rearrange("(e p) s -> p e s", p=P), res[:])
 
         share(0)
+        finish(0, P, z_first[0], (0, 3))
+        z1 = mix(0)
+        finish(P, P, z_first[1], (1, 4))
         share(1)
-        z0 = mix(0)
-        nc.vector.quantize_mx(out=w2_codes[:].bitcast(FP8X4), scales=w2_sc[:], in_=w2_bf[:].rearrange("p n t -> p (n t)"))
-        finish(0, z0, 0)
-        z1 = mix(1)
-        share(2)
-        finish(1, z1, 2)
-        z2 = mix(2)
-        finish(2, z2, 4)
+        finish(HALF, P, z1, (5, 6))
+        z2 = mix(1)
+        finish(HALF + P, P, z2, (7, 2, 0, 3))

@@ -114,7 +114,7 @@ def tile_picked_cmpex_none_p_kernel(tc, x_words, x_scales, w1, up, w2, offs, mat
         sums = [psum.tile([P, PACK, P], F32, name="sum_bank", tag="bank%d" % c) for c in range(2)]
 
         def add_turned(c, t, source, start=False, stop=False):
-            nc.tensor.matmul(sums[c][:, t, :], source[:, P * c : P * c + P], ident[:], is_transpose=True, start=start, stop=stop)
+            nc.tensor.matmul(sums[c][:, 2 * (t % 2) + t // 2, :], source[:, P * c : P * c + P], ident[:], is_transpose=True, start=start, stop=stop)
 
         for t in range(PACK):
             for c in range(2):
@@ -132,8 +132,8 @@ def tile_picked_cmpex_none_p_kernel(tc, x_words, x_scales, w1, up, w2, offs, mat
         nc.scalar.activation(gap2[:, 2:4, :], diffs[1][:, :, second], ACT.Abs)
         for planes in (slice(0, 3), slice(3, 4)):
             nc.vector.scalar_tensor_tensor(slope[:, planes, :], up_sb[:, planes, first], 0.5, gap1[:, planes, :], ALU.subtract, ALU.mult)
-        for t in range(PACK):
-            for c in range(2):
+        for c in range(2):
+            for t in range(PACK):
                 add_turned(c, t, slope[:, t, :], stop=t == PACK - 1)
 
         part = up_sb[:, :, first]
@@ -146,23 +146,31 @@ def tile_picked_cmpex_none_p_kernel(tc, x_words, x_scales, w1, up, w2, offs, mat
                     lo[:, t, c0 - HALF : piece.stop - HALF], diffs[t // 2][:, t % 2, c0 : piece.stop], 0.0, bank[:, c0 - piece.start :], ALU.min, ALU.add
                 )
 
+        w2_cuts = [(0, P), (P, HALF), (HALF, N)]
         w2_bf = [
-            keep.tile([P, HALF, PACK], BF16, name="w2_bf%d" % u, tag=tag, align_bytes=64) for u, tag in enumerate(("last_plain", "diff0"))
+            keep.tile([P, P, PACK], BF16, name="w2_bf0", tag="last_plain", align_bytes=64),
+            keep.tile([P, N - P, PACK], BF16, name="w2_bf1", tag="diff0", align_bytes=64),
         ]
-        for u, copy in enumerate((nc.scalar.copy, nc.vector.tensor_copy)):
+        for copy, dealt, cols in ((nc.scalar.copy, w2_bf[0], slice(0, P)), (nc.vector.tensor_copy, w2_bf[1], slice(P, N))):
             copy(
-                w2_bf[u][:].rearrange("p (c i) t -> p c t i", i=2),
-                w2_raw[:, :, halves[u]].rearrange("p t (c i) -> p c t i", i=2),
+                dealt[:].rearrange("p (c i) t -> p c t i", i=4),
+                w2_raw[:, :, cols].rearrange("p t (c i) -> p c t i", i=4),
             )
         w2_codes = keep.tile([P, N], U32, name="w2_codes", tag="diff1", align_bytes=64)
         w2_sc = keep.tile([P, N], U8, name="w2_sc", align_bytes=64)
-        for u in range(2):
-            nc.vector.quantize_mx(out=w2_codes[:, halves[u]].bitcast(FP8X4), scales=w2_sc[:, halves[u]], in_=w2_bf[u][:].rearrange("p n t -> p (n t)"))
+        for c0, c1 in w2_cuts:
+            dealt = w2_bf[0][:] if c0 == 0 else w2_bf[1][:, c0 - P : c1 - P, :]
+            nc.vector.quantize_mx(out=w2_codes[:, c0:c1].bitcast(FP8X4), scales=w2_sc[:, c0:c1], in_=dealt.rearrange("p n t -> p (n t)"))
 
         backs = []
         for c, tag in enumerate(("bank7", "bank2")):
             turned = keep.tile([P, 2, P, 2], BF16, name="turned%d" % c)
-            nc.scalar.activation(turned[:], sums[c][:].rearrange("j (u e) p -> j u p e", e=2), ACT.Copy, scale=0.5)
+            nc.scalar.activation(
+                turned[:].rearrange("j u (q i) e -> j (u q) e i", i=4),
+                sums[c][:].rearrange("j (e u) (q i) -> j (u q) e i", e=2, i=4),
+                ACT.Copy,
+                scale=0.5,
+            )
             words = turned[:].rearrange("j u p e -> j u (p e)").bitcast(F32)
             back = psum.tile([P, 2, P], F32, name="back_bank", tag=tag)
             for u in range(2):
@@ -172,8 +180,8 @@ def tile_picked_cmpex_none_p_kernel(tc, x_words, x_scales, w1, up, w2, offs, mat
         for c in range(2):
             z_bf = keep.tile([P, P, PACK], BF16, name="z_first%d" % c, align_bytes=64)
             nc.scalar.copy(
-                z_bf[:].rearrange("p n t -> p (n t)").bitcast(F32).rearrange("p (j u) -> p j u", u=2),
-                backs[c][:].rearrange("p u j -> p j u"),
+                z_bf[:].rearrange("p n t -> p (n t)").bitcast(F32).rearrange("p (q i u) -> p q u i", i=4, u=2),
+                backs[c][:].rearrange("p u (q i) -> p q u i", i=4),
             )
             z_first.append(z_bf)
 
@@ -198,6 +206,8 @@ def tile_picked_cmpex_none_p_kernel(tc, x_words, x_scales, w1, up, w2, offs, mat
             sc = keep.tile([P, n], U8, name="z_sc%d" % c0, align_bytes=64)
             nc.vector.quantize_mx(out=codes[:].bitcast(FP8X4), scales=sc[:], in_=z_bf[:].rearrange("p n t -> p (n t)"))
             rows = 1 if last else 2
+            joined = 0 < c0 and not last
+            res = keep.tile([P, PACK, n], F32, name="res%d" % c0) if joined else None
             for b in range(PACK // rows):
                 bank = psum.tile([P, rows, n], F32, name="o_bank", tag="bank%d" % banks[b])
                 for e in range(rows):
@@ -211,6 +221,9 @@ def tile_picked_cmpex_none_p_kernel(tc, x_words, x_scales, w1, up, w2, offs, mat
                         start=True,
                         stop=True,
                     )
+                if joined:
+                    nc.scalar.copy(res[:, rows * b : rows * (b + 1), :], bank[:])
+                    continue
                 res = keep.tile([P, rows, n], F32, name="res%d_%d" % (c0, b))
                 by_vector = last and b % 2 == 1
                 if by_vector:
@@ -219,11 +232,13 @@ def tile_picked_cmpex_none_p_kernel(tc, x_words, x_scales, w1, up, w2, offs, mat
                     nc.scalar.copy(res[:], bank[:])
                 queue = nc.scalar if last and b >= 2 else nc.sync
                 queue.dma_start(out[rows * P * b : rows * P * (b + 1), c0 : c0 + n].rearrange("(e p) s -> p e s", p=P), res[:])
+            if joined:
+                nc.sync.dma_start(out[:, c0 : c0 + n].rearrange("(e p) s -> p e s", p=P), res[:])
 
-        share(0)
         finish(0, P, z_first[0], (0, 3))
-        z1 = mix(0)
+        share(0)
         finish(P, P, z_first[1], (1, 4))
+        z1 = mix(0)
         share(1)
         finish(HALF, P, z1, (5, 6))
         z2 = mix(1)

@@ -122,23 +122,24 @@ def tile_picked_cmpex_none_p_kernel(tc, x_words, x_scales, w1, up, w2, offs, mat
                 add_turned(c, t, plains[t])
                 add_turned(c, t, diffs[t // 2][:, t % 2, :])
 
-        gap1 = keep.tile([P, PACK, HALF], F32, name="gap1", tag="gap1")
+        gap1 = keep.tile([P, PACK, HALF], F32, name="gap1")
+        gap_last = keep.tile([P, HALF], F32, name="gap_last", tag="gap_last")
         gap2 = keep.tile([P, PACK, HALF], F32, name="gap2")
         slope = keep.tile([P, PACK, HALF], F32, name="slope")
         nc.scalar.activation(gap1[:, 0:2, :], diffs[0][:, :, first], ACT.Abs, scale=2.0)
         nc.scalar.activation(gap1[:, 2, :], diffs[1][:, 0, first], ACT.Abs, scale=2.0)
         nc.scalar.activation(gap2[:, 0:2, :], diffs[0][:, :, second], ACT.Abs)
-        nc.scalar.activation(gap1[:, 3, :], diffs[1][:, 1, first], ACT.Abs, scale=2.0)
+        nc.scalar.activation(gap_last[:], diffs[1][:, 1, first], ACT.Abs, scale=2.0)
         nc.scalar.activation(gap2[:, 2:4, :], diffs[1][:, :, second], ACT.Abs)
-        for planes in (slice(0, 3), slice(3, 4)):
-            nc.vector.scalar_tensor_tensor(slope[:, planes, :], up_sb[:, planes, first], 0.5, gap1[:, planes, :], ALU.subtract, ALU.mult)
+        nc.vector.scalar_tensor_tensor(slope[:, 0:3, :], up_sb[:, 0:3, first], 0.5, gap1[:, 0:3, :], ALU.subtract, ALU.mult)
+        nc.vector.scalar_tensor_tensor(slope[:, 3, :], up_sb[:, 3, first], 0.5, gap_last[:], ALU.subtract, ALU.mult)
         for c in range(2):
             for t in range(PACK):
                 add_turned(c, t, slope[:, t, :], stop=t == PACK - 1)
 
-        part = up_sb[:, :, first]
-        nc.gpsimd.tensor_tensor(part[:, 2:4, :], gap2[:, 2:4, :], up_sb[:, 2:4, second], ALU.mult)
-        lo = keep.tile([P, PACK, HALF], F32, name="lo", tag="gap1")
+        part = gap1
+        nc.gpsimd.tensor_tensor(part[:, 0:2, :], gap2[:, 0:2, :], up_sb[:, 0:2, second], ALU.mult)
+        lo = keep.tile([P, PACK, HALF], F32, name="lo", tag="gap_last")
         for t, piece, bank in y_banks:
             if piece.stop > HALF:
                 c0 = max(piece.start, HALF)
@@ -146,21 +147,18 @@ def tile_picked_cmpex_none_p_kernel(tc, x_words, x_scales, w1, up, w2, offs, mat
                     lo[:, t, c0 - HALF : piece.stop - HALF], diffs[t // 2][:, t % 2, c0 : piece.stop], 0.0, bank[:, c0 - piece.start :], ALU.min, ALU.add
                 )
 
-        w2_cuts = [(0, P), (P, HALF), (HALF, N)]
         w2_bf = [
-            keep.tile([P, P, PACK], BF16, name="w2_bf0", tag="last_plain", align_bytes=64),
-            keep.tile([P, N - P, PACK], BF16, name="w2_bf1", tag="diff0", align_bytes=64),
+            keep.tile([P, HALF, PACK], BF16, name="w2_bf%d" % u, tag=tag, align_bytes=64) for u, tag in enumerate(("last_plain", "diff0"))
         ]
-        for copy, dealt, cols in ((nc.scalar.copy, w2_bf[0], slice(0, P)), (nc.vector.tensor_copy, w2_bf[1], slice(P, N))):
+        for u, copy in enumerate((nc.scalar.copy, nc.vector.tensor_copy)):
             copy(
-                dealt[:].rearrange("p (c i) t -> p c t i", i=4),
-                w2_raw[:, :, cols].rearrange("p t (c i) -> p c t i", i=4),
+                w2_bf[u][:].rearrange("p (c i) t -> p c t i", i=4),
+                w2_raw[:, :, halves[u]].rearrange("p t (c i) -> p c t i", i=4),
             )
         w2_codes = keep.tile([P, N], U32, name="w2_codes", tag="diff1", align_bytes=64)
         w2_sc = keep.tile([P, N], U8, name="w2_sc", align_bytes=64)
-        for c0, c1 in w2_cuts:
-            dealt = w2_bf[0][:] if c0 == 0 else w2_bf[1][:, c0 - P : c1 - P, :]
-            nc.vector.quantize_mx(out=w2_codes[:, c0:c1].bitcast(FP8X4), scales=w2_sc[:, c0:c1], in_=dealt.rearrange("p n t -> p (n t)"))
+        for u in range(2):
+            nc.vector.quantize_mx(out=w2_codes[:, halves[u]].bitcast(FP8X4), scales=w2_sc[:, halves[u]], in_=w2_bf[u][:].rearrange("p n t -> p (n t)"))
 
         backs = []
         for c, tag in enumerate(("bank7", "bank2")):
@@ -187,7 +185,7 @@ def tile_picked_cmpex_none_p_kernel(tc, x_words, x_scales, w1, up, w2, offs, mat
 
         def share(c):
             cols = slice(P * c, P * c + P)
-            nc.vector.tensor_tensor(part[:, 0:2, cols], gap2[:, 0:2, cols], up_sb[:, 0:2, HALF + P * c : HALF + P * c + P], ALU.mult)
+            nc.vector.tensor_tensor(part[:, 2:4, cols], gap2[:, 2:4, cols], up_sb[:, 2:4, HALF + P * c : HALF + P * c + P], ALU.mult)
 
         def mix(c):
             cols = slice(P * c, P * c + P)
@@ -235,10 +233,10 @@ def tile_picked_cmpex_none_p_kernel(tc, x_words, x_scales, w1, up, w2, offs, mat
             if joined:
                 nc.sync.dma_start(out[:, c0 : c0 + n].rearrange("(e p) s -> p e s", p=P), res[:])
 
-        finish(0, P, z_first[0], (0, 3))
         share(0)
-        finish(P, P, z_first[1], (1, 4))
+        finish(0, P, z_first[0], (0, 3))
         z1 = mix(0)
+        finish(P, P, z_first[1], (1, 4))
         share(1)
         finish(HALF, P, z1, (5, 6))
         z2 = mix(1)

@@ -203,13 +203,10 @@ def tile_picked_cmpex_none_p_kernel(tc, x_words, x_scales, w1, up, w2, offs, mat
             codes = keep.tile([P, n], U32, name="z_codes%d" % c0, align_bytes=64)
             sc = keep.tile([P, n], U8, name="z_sc%d" % c0, align_bytes=64)
             nc.vector.quantize_mx(out=codes[:].bitcast(FP8X4), scales=sc[:], in_=z_bf[:].rearrange("p n t -> p (n t)"))
-            rows = 1 if last else 2
-            joined = 0 < c0 and not last
-            res = keep.tile([P, PACK, n], F32, name="res%d" % c0) if joined else None
-            for b in range(PACK // rows):
-                bank = psum.tile([P, rows, n], F32, name="o_bank", tag="bank%d" % banks[b])
-                for e in range(rows):
-                    cols = slice(P * (rows * b + e), P * (rows * b + e) + P)
+            for b in range(2):
+                bank = psum.tile([P, 2, n], F32, name="o_bank", tag="bank%d" % banks[b])
+                for e in range(2):
+                    cols = slice(P * (2 * b + e), P * (2 * b + e) + P)
                     nc.tensor.matmul_mx(
                         out=bank[:, e, :],
                         lhsT=w2_codes[:, cols].bitcast(FP8X4),
@@ -219,19 +216,13 @@ def tile_picked_cmpex_none_p_kernel(tc, x_words, x_scales, w1, up, w2, offs, mat
                         start=True,
                         stop=True,
                     )
-                if joined:
-                    nc.scalar.copy(res[:, rows * b : rows * (b + 1), :], bank[:])
-                    continue
-                res = keep.tile([P, rows, n], F32, name="res%d_%d" % (c0, b))
-                by_vector = last and b % 2 == 1
-                if by_vector:
+                res = keep.tile([P, 2, n], F32, name="res%d_%d" % (c0, b))
+                if last and b == 1:
                     nc.vector.tensor_copy(res[:], bank[:])
                 else:
                     nc.scalar.copy(res[:], bank[:])
-                queue = nc.scalar if last and b >= 2 else nc.sync
-                queue.dma_start(out[rows * P * b : rows * P * (b + 1), c0 : c0 + n].rearrange("(e p) s -> p e s", p=P), res[:])
-            if joined:
-                nc.sync.dma_start(out[:, c0 : c0 + n].rearrange("(e p) s -> p e s", p=P), res[:])
+                queue = nc.scalar if last and b == 0 else nc.sync
+                queue.dma_start(out[2 * P * b : 2 * P * (b + 1), c0 : c0 + n].rearrange("(e p) s -> p e s", p=P), res[:])
 
         share(0)
         finish(0, P, z_first[0], (0, 3))
@@ -240,4 +231,4 @@ def tile_picked_cmpex_none_p_kernel(tc, x_words, x_scales, w1, up, w2, offs, mat
         share(1)
         finish(HALF, P, z1, (5, 6))
         z2 = mix(1)
-        finish(HALF + P, P, z2, (7, 2, 0, 3))
+        finish(HALF + P, P, z2, (7, 2))

@@ -53,11 +53,12 @@ def tile_picked_cmpex_none_p_kernel(tc, x_words, x_scales, w1, up, w2, offs, mat
         for u in (1, 0):
             nc.vector.quantize_mx(out=w1_codes[u][:].bitcast(FP8X4), scales=w1_sc[u][:], in_=w1_bf[u][:].rearrange("p e m j -> p (e m j)"))
 
-        late = keep.tile([P, 2 * PACK, H], F32, name="late", tag="raw")
-        up_sb = late[:, 0:PACK, :]
-        w2_raw = late[:, PACK : 2 * PACK, :]
+        late = keep.tile([P, 2 * PACK * S], F32, name="late", tag="raw")
+        w2_raw = [late[:, PACK * HALF * u : PACK * HALF * (u + 1)].rearrange("p (t n) -> p t n", t=PACK) for u in range(2)]
+        up_sb = late[:, PACK * S : 2 * PACK * S].rearrange("p (t s) -> p t s", t=PACK)
+        for u in range(2):
+            nc.sync.dma_start(w2_raw[u], w2.rearrange("(p t) n -> p t n", t=PACK)[:, :, halves[u]])
         nc.sync.dma_start(up_sb, up.rearrange("(p t) s -> p t s", t=PACK))
-        nc.sync.dma_start(w2_raw, w2.rearrange("(p t) n -> p t n", t=PACK))
 
         x_codes = keep.tile([P, S], U32, name="x_codes", align_bytes=64)
         for h in range(2):
@@ -65,16 +66,20 @@ def tile_picked_cmpex_none_p_kernel(tc, x_words, x_scales, w1, up, w2, offs, mat
 
         ident = keep.tile([P, P], F32, name="ident")
         make_identity(nc, ident[:])
-        diffs = [keep.tile([P, 2, S], F32, name="diff%d" % u, tag="diff%d" % u, align_bytes=64) for u in range(2)]
-        tables = [keep.tile([P, S if t == 0 else 2 * S], F32, name="y_table%d" % t, tag="table%d" % t) for t in range(PACK)]
-        last_plain = keep.tile([P, S], F32, name="last_plain", tag="last_plain", align_bytes=64)
-        plains = [tables[t + 1][:, S : 2 * S] if t + 1 < PACK else last_plain[:] for t in range(PACK)]
-        y_banks = []
+        first, second = halves
+        lo = up_sb[:, :, first]
+        tables = [keep.tile([P, S], F32, name="y_table%d" % t) for t in range(PACK)]
+        plains = [keep.tile([P, HALF], F32, name="plain%d" % t, tag="plain%d" % t, align_bytes=64) for t in range(PACK)]
+        near = keep.tile([P, PACK, HALF], F32, name="near")
+        other = keep.tile([P, PACK, HALF], F32, name="other")
+        far = keep.tile([P, PACK, HALF], F32, name="far")
+        gap1 = keep.tile([P, PACK, HALF], F32, name="gap1")
+        gap2 = keep.tile([P, PACK, HALF], F32, name="gap2")
+        slope = keep.tile([P, PACK, HALF], F32, name="slope")
 
-        def product(t, piece):
+        def product(b, t, piece):
             cols = slice(P * (t % 2), P * (t % 2) + P)
-            bank = psum.tile([P, piece.stop - piece.start], F32, name="y_bank", tag="bank%d" % len(y_banks))
-            y_banks.append((t, piece, bank))
+            bank = psum.tile([P, piece.stop - piece.start], F32, name="y_bank", tag="bank%d" % b)
             nc.tensor.matmul_mx(
                 out=bank[:],
                 lhsT=w1_codes[t // 2][:, cols].bitcast(FP8X4),
@@ -86,31 +91,43 @@ def tile_picked_cmpex_none_p_kernel(tc, x_words, x_scales, w1, up, w2, offs, mat
             )
             return bank
 
-        def fetch(t, piece):
-            mates = mate_sb[:, piece.start // 16 : piece.stop // 16]
-            nc.vector.tensor_tensor(diffs[t // 2][:, t % 2, piece], tables[t][:].indirect(mates), plains[t][:, piece], ALU.subtract)
+        def round_w2(u, tag):
+            w2_bf = keep.tile([P, HALF, PACK], BF16, name="w2_bf%d" % u, tag=tag, align_bytes=64)
+            nc.gpsimd.tensor_scalar(w2_bf[:], w2_raw[u].rearrange("p t n -> p n t"), 1.0, 0.0, ALU.mult, ALU.add)
+            return w2_bf
 
-        early = [product(t, halves[0]) for t in range(2)]
-        nc.scalar.copy(tables[0][:, halves[0]], early[0][:])
-        quarters = [slice(HALF, HALF + P), slice(HALF + P, S)]
-        rest = [product(0, piece) for piece in quarters]
-        for piece, bank in zip(quarters, rest):
-            nc.scalar.copy(tables[0][:, piece], bank[:])
-        for t in range(2):
-            nc.vector.tensor_copy(plains[t][:, halves[0]], early[t][:])
-        for piece, bank in zip(quarters, rest):
-            nc.scalar.copy(plains[0][:, piece], bank[:])
-        for piece in halves:
-            fetch(0, piece)
-        nc.scalar.copy(tables[1][:, halves[0]], early[1][:])
-        for t in range(1, PACK):
-            piece = halves[1] if t == 1 else slice(0, S)
-            bank = product(t, piece)
-            nc.scalar.copy(tables[t][:, piece], bank[:])
-            nc.scalar.copy(plains[t][:, piece], bank[:])
-            fetch(t, slice(0, S))
+        def fetch_near(t):
+            nc.vector.tensor_tensor(near[:, t, :], tables[t][:].indirect(mate_sb[:, 0:16]), plains[t][:], ALU.subtract)
 
-        first, second = halves
+        def fetch_other(t):
+            nc.scalar.activation(other[:, t, :], tables[t][:].indirect(mate_sb[:, 16:32]), ACT.Copy)
+
+        def differ(t):
+            nc.vector.tensor_tensor(far[:, t, :], other[:, t, :], y_far[t], ALU.subtract)
+
+        def lesser(t):
+            nc.vector.tensor_tensor(lo[:, t, :], other[:, t, :], y_far[t], ALU.min)
+
+        banks = [product(0, 0, first), product(1, 1, first), product(2, 0, second), product(3, 1, second), product(4, 2, slice(0, S)), product(5, 3, slice(0, S))]
+        y_far = [banks[2][:], banks[3][:], banks[4][:, second], banks[5][:, second]]
+        w2_bf = [round_w2(0, "w2_first")]
+        nc.scalar.copy(tables[0][:, first], banks[0][:])
+        nc.vector.tensor_copy(tables[1][:, first], banks[1][:])
+        nc.vector.tensor_copy(plains[1][:], banks[1][:])
+        nc.scalar.copy(tables[0][:, second], banks[2][:])
+        nc.vector.tensor_copy(tables[1][:, second], banks[3][:])
+        nc.vector.tensor_copy(plains[0][:], banks[0][:])
+        fetch_other(0)
+        for t in (2, 3):
+            nc.scalar.copy(tables[t][:], banks[t + 2][:])
+        for t in (0, 1):
+            fetch_near(t)
+        for t in (2, 3):
+            nc.vector.tensor_copy(plains[t][:], tables[t][:, first])
+        for t in (2, 3):
+            fetch_near(t)
+        w2_bf.append(round_w2(1, "plain2"))
+
         sums = [psum.tile([P, PACK, P], F32, name="sum_bank", tag="bank%d" % c) for c in range(2)]
 
         def add_turned(c, t, source, start=False, stop=False):
@@ -118,50 +135,36 @@ def tile_picked_cmpex_none_p_kernel(tc, x_words, x_scales, w1, up, w2, offs, mat
 
         for t in range(PACK):
             for c in range(2):
-                add_turned(c, t, tables[t][:, 0:S], start=t == 0)
-                add_turned(c, t, plains[t])
-                add_turned(c, t, diffs[t // 2][:, t % 2, :])
+                add_turned(c, t, tables[t][:, first], start=t == 0)
+                add_turned(c, t, tables[t][:, first])
+                add_turned(c, t, near[:, t, :])
 
-        gap1 = keep.tile([P, PACK, HALF], F32, name="gap1")
-        gap_last = keep.tile([P, HALF], F32, name="gap_last", tag="gap_last")
-        gap2 = keep.tile([P, PACK, HALF], F32, name="gap2")
-        slope = keep.tile([P, PACK, HALF], F32, name="slope")
-        nc.scalar.activation(gap1[:, 0:2, :], diffs[0][:, :, first], ACT.Abs, scale=2.0)
-        nc.scalar.activation(gap1[:, 2, :], diffs[1][:, 0, first], ACT.Abs, scale=2.0)
-        nc.scalar.activation(gap2[:, 0:2, :], diffs[0][:, :, second], ACT.Abs)
-        nc.scalar.activation(gap_last[:], diffs[1][:, 1, first], ACT.Abs, scale=2.0)
-        nc.scalar.activation(gap2[:, 2:4, :], diffs[1][:, :, second], ACT.Abs)
-        nc.vector.scalar_tensor_tensor(slope[:, 0:3, :], up_sb[:, 0:3, first], 0.5, gap1[:, 0:3, :], ALU.subtract, ALU.mult)
-        nc.vector.scalar_tensor_tensor(slope[:, 3, :], up_sb[:, 3, first], 0.5, gap_last[:], ALU.subtract, ALU.mult)
+        for t in range(1, PACK):
+            fetch_other(t)
+        pairs = [slice(0, 2), slice(2, 4)]
+        for planes in pairs:
+            nc.scalar.activation(gap1[:, planes, :], near[:, planes, :], ACT.Abs, scale=2.0)
+        for t in range(PACK):
+            differ(t)
+        for planes in pairs:
+            nc.scalar.activation(gap2[:, planes, :], far[:, planes, :], ACT.Abs)
+            nc.vector.scalar_tensor_tensor(slope[:, planes, :], up_sb[:, planes, first], 0.5, gap1[:, planes, :], ALU.subtract, ALU.mult)
         for c in range(2):
             for t in range(PACK):
                 add_turned(c, t, slope[:, t, :], stop=t == PACK - 1)
 
         part = gap1
         nc.gpsimd.tensor_tensor(part[:, 0:2, :], gap2[:, 0:2, :], up_sb[:, 0:2, second], ALU.mult)
-        lo = keep.tile([P, PACK, HALF], F32, name="lo", tag="gap_last")
-        for t, piece, bank in y_banks:
-            if piece.stop > HALF:
-                c0 = max(piece.start, HALF)
-                nc.vector.scalar_tensor_tensor(
-                    lo[:, t, c0 - HALF : piece.stop - HALF], diffs[t // 2][:, t % 2, c0 : piece.stop], 0.0, bank[:, c0 - piece.start :], ALU.min, ALU.add
-                )
+        for t in range(PACK):
+            lesser(t)
 
-        w2_bf = [
-            keep.tile([P, HALF, PACK], BF16, name="w2_bf%d" % u, tag=tag, align_bytes=64) for u, tag in enumerate(("last_plain", "diff0"))
-        ]
-        for u, copy in enumerate((nc.scalar.copy, nc.vector.tensor_copy)):
-            copy(
-                w2_bf[u][:].rearrange("p (c i) t -> p c t i", i=4),
-                w2_raw[:, :, halves[u]].rearrange("p t (c i) -> p c t i", i=4),
-            )
-        w2_codes = keep.tile([P, N], U32, name="w2_codes", tag="diff1", align_bytes=64)
+        w2_codes = keep.tile([P, N], U32, name="w2_codes", align_bytes=64)
         w2_sc = keep.tile([P, N], U8, name="w2_sc", align_bytes=64)
         for u in range(2):
             nc.vector.quantize_mx(out=w2_codes[:, halves[u]].bitcast(FP8X4), scales=w2_sc[:, halves[u]], in_=w2_bf[u][:].rearrange("p n t -> p (n t)"))
 
         backs = []
-        for c, tag in enumerate(("bank7", "bank2")):
+        for c, tag in enumerate(("bank6", "bank7")):
             turned = keep.tile([P, 2, P, 2], BF16, name="turned%d" % c)
             nc.scalar.activation(
                 turned[:].rearrange("j u (q i) e -> j (u q) e i", i=4),
@@ -225,10 +228,10 @@ def tile_picked_cmpex_none_p_kernel(tc, x_words, x_scales, w1, up, w2, offs, mat
                 queue.dma_start(out[2 * P * b : 2 * P * (b + 1), c0 : c0 + n].rearrange("(e p) s -> p e s", p=P), res[:])
 
         share(0)
-        finish(0, P, z_first[0], (0, 3))
+        finish(0, P, z_first[0], (2, 3))
         z1 = mix(0)
-        finish(P, P, z_first[1], (1, 4))
+        finish(P, P, z_first[1], (4, 5))
         share(1)
-        finish(HALF, P, z1, (5, 6))
+        finish(HALF, P, z1, (0, 1))
         z2 = mix(1)
-        finish(HALF + P, P, z2, (7, 2))
+        finish(HALF + P, P, z2, (6, 7))

@@ -36,7 +36,7 @@ def tile_picked_cmpex_none_p_kernel(tc, x_words, x_scales, w1, up, w2, offs, mat
         nc.sync.dma_start(w1_raw[:], w1.rearrange("(p j) c -> p j c", j=PACK))
         for q in range(4):
             nc.sync.dma_start(scale_table[32 * q : 32 * q + 4, :].bitcast(I32), x_scales[0, 4 * q : 4 * q + 4, :].bitcast(I32))
-        x_table = keep.tile([P, T], U32, name="x_table", align_bytes=64)
+        x_table = keep.tile([P, T], U32, name="x_table", tag="x_table", align_bytes=64)
         nc.sync.dma_start(x_table[:].bitcast(I32), x_words[0].rearrange("p n t -> p (n t)").bitcast(I32))
         mate_sb = keep.tile([P, S // 16], U16, name="mate_sb")
         nc.sync.dma_start(mate_sb[:], mate)
@@ -53,12 +53,14 @@ def tile_picked_cmpex_none_p_kernel(tc, x_words, x_scales, w1, up, w2, offs, mat
         for u in (1, 0):
             nc.vector.quantize_mx(out=w1_codes[u][:].bitcast(FP8X4), scales=w1_sc[u][:], in_=w1_bf[u][:].rearrange("p e m j -> p (e m j)"))
 
-        late = keep.tile([P, 2 * PACK * S], F32, name="late", tag="raw")
-        w2_raw = [late[:, PACK * HALF * u : PACK * HALF * (u + 1)].rearrange("p (t n) -> p t n", t=PACK) for u in range(2)]
-        up_sb = late[:, PACK * S : 2 * PACK * S].rearrange("p (t s) -> p t s", t=PACK)
-        for u in range(2):
-            nc.sync.dma_start(w2_raw[u], w2.rearrange("(p t) n -> p t n", t=PACK)[:, :, halves[u]])
+        w2_rows = w2.rearrange("(p t) n -> p t n", t=PACK)
+        w2_early = keep.tile([P, PACK, HALF], F32, name="w2_early")
+        nc.sync.dma_start(w2_early[:], w2_rows[:, :, halves[0]])
+        late = keep.tile([P, PACK * (S + HALF)], F32, name="late", tag="raw")
+        up_sb = late[:, 0 : PACK * S].rearrange("p (t s) -> p t s", t=PACK)
+        w2_raw = [w2_early[:], late[:, PACK * S :].rearrange("p (t n) -> p t n", t=PACK)]
         nc.sync.dma_start(up_sb, up.rearrange("(p t) s -> p t s", t=PACK))
+        nc.sync.dma_start(w2_raw[1], w2_rows[:, :, halves[1]])
 
         x_codes = keep.tile([P, S], U32, name="x_codes", align_bytes=64)
         for h in range(2):
@@ -69,12 +71,15 @@ def tile_picked_cmpex_none_p_kernel(tc, x_words, x_scales, w1, up, w2, offs, mat
         first, second = halves
         lo = up_sb[:, :, first]
         tables = [keep.tile([P, S], F32, name="y_table%d" % t) for t in range(PACK)]
-        plains = [keep.tile([P, HALF], F32, name="plain%d" % t, tag="plain%d" % t, align_bytes=64) for t in range(PACK)]
+        plains = [keep.tile([P, HALF], F32, name="plain%d" % t, tag="plain%d" % t, align_bytes=64) for t in range(PACK - 1)]
+        near_last = keep.tile([P, HALF], F32, name="near_last")
         near = keep.tile([P, PACK, HALF], F32, name="near")
-        other = keep.tile([P, PACK, HALF], F32, name="other")
-        far = keep.tile([P, PACK, HALF], F32, name="far")
+        other_first = keep.tile([P, PACK - 1, HALF], F32, name="other_first")
+        other = [other_first[:, 0, :], other_first[:, 1, :], other_first[:, 2, :], near[:, 3, :]]
+        far = keep.tile([P, PACK, HALF], F32, name="far", tag="far", align_bytes=64)
         gap1 = keep.tile([P, PACK, HALF], F32, name="gap1")
-        gap2 = keep.tile([P, PACK, HALF], F32, name="gap2")
+        gap_last = keep.tile([P, 2, HALF], F32, name="gap_last")
+        gap2 = [near[:, 1:3, :], gap_last[:]]
         slope = keep.tile([P, PACK, HALF], F32, name="slope")
 
         def product(b, t, piece):
@@ -100,33 +105,34 @@ def tile_picked_cmpex_none_p_kernel(tc, x_words, x_scales, w1, up, w2, offs, mat
             nc.vector.tensor_tensor(near[:, t, :], tables[t][:].indirect(mate_sb[:, 0:16]), plains[t][:], ALU.subtract)
 
         def fetch_other(t):
-            nc.scalar.activation(other[:, t, :], tables[t][:].indirect(mate_sb[:, 16:32]), ACT.Copy)
+            nc.scalar.activation(other[t], tables[t][:].indirect(mate_sb[:, 16:32]), ACT.Copy)
 
         def differ(t):
-            nc.vector.tensor_tensor(far[:, t, :], other[:, t, :], y_far[t], ALU.subtract)
+            nc.vector.tensor_tensor(far[:, t, :], other[t], y_far[t], ALU.subtract)
 
         def lesser(t):
-            nc.vector.tensor_tensor(lo[:, t, :], other[:, t, :], y_far[t], ALU.min)
+            nc.vector.tensor_tensor(lo[:, t, :], other[t], y_far[t], ALU.min)
 
         banks = [product(0, 0, first), product(1, 1, first), product(2, 0, second), product(3, 1, second), product(4, 2, slice(0, S)), product(5, 3, slice(0, S))]
         y_far = [banks[2][:], banks[3][:], banks[4][:, second], banks[5][:, second]]
-        w2_bf = [round_w2(0, "w2_first")]
+        w2_bf = [round_w2(0, "x_table")]
         nc.scalar.copy(tables[0][:, first], banks[0][:])
         nc.vector.tensor_copy(tables[1][:, first], banks[1][:])
         nc.vector.tensor_copy(plains[1][:], banks[1][:])
         nc.scalar.copy(tables[0][:, second], banks[2][:])
         nc.vector.tensor_copy(tables[1][:, second], banks[3][:])
         nc.vector.tensor_copy(plains[0][:], banks[0][:])
-        fetch_other(0)
-        for t in (2, 3):
-            nc.scalar.copy(tables[t][:], banks[t + 2][:])
+        nc.vector.tensor_copy(tables[2][:], banks[4][:])
         for t in (0, 1):
-            fetch_near(t)
-        for t in (2, 3):
-            nc.vector.tensor_copy(plains[t][:], tables[t][:, first])
-        for t in (2, 3):
+            fetch_other(t)
+        nc.scalar.copy(tables[3][:], banks[5][:])
+        nc.scalar.activation(near_last[:], tables[3][:].indirect(mate_sb[:, 0:16]), ACT.Copy)
+        fetch_near(0)
+        nc.vector.tensor_copy(plains[2][:], tables[2][:, first])
+        for t in (1, 2):
             fetch_near(t)
         w2_bf.append(round_w2(1, "plain2"))
+        nc.vector.tensor_tensor(near[:, 3, :], near_last[:], banks[5][:, first], ALU.subtract)
 
         sums = [psum.tile([P, PACK, P], F32, name="sum_bank", tag="bank%d" % c) for c in range(2)]
 
@@ -136,29 +142,34 @@ def tile_picked_cmpex_none_p_kernel(tc, x_words, x_scales, w1, up, w2, offs, mat
         for t in range(PACK):
             for c in range(2):
                 add_turned(c, t, tables[t][:, first], start=t == 0)
-                add_turned(c, t, tables[t][:, first])
-                add_turned(c, t, near[:, t, :])
+                if t < PACK - 1:
+                    add_turned(c, t, tables[t][:, first])
+                    add_turned(c, t, near[:, t, :])
+                else:
+                    add_turned(c, t, near_last[:])
 
-        for t in range(1, PACK):
-            fetch_other(t)
+        fetch_other(2)
         pairs = [slice(0, 2), slice(2, 4)]
         for planes in pairs:
             nc.scalar.activation(gap1[:, planes, :], near[:, planes, :], ACT.Abs, scale=2.0)
-        for t in range(PACK):
+        fetch_other(3)
+        for t in range(PACK - 1):
             differ(t)
         for planes in pairs:
-            nc.scalar.activation(gap2[:, planes, :], far[:, planes, :], ACT.Abs)
             nc.vector.scalar_tensor_tensor(slope[:, planes, :], up_sb[:, planes, first], 0.5, gap1[:, planes, :], ALU.subtract, ALU.mult)
+        differ(3)
+        for u, planes in enumerate(pairs):
+            nc.scalar.activation(gap2[u], far[:, planes, :], ACT.Abs)
         for c in range(2):
             for t in range(PACK):
                 add_turned(c, t, slope[:, t, :], stop=t == PACK - 1)
 
         part = gap1
-        nc.gpsimd.tensor_tensor(part[:, 0:2, :], gap2[:, 0:2, :], up_sb[:, 0:2, second], ALU.mult)
+        nc.gpsimd.tensor_tensor(part[:, 0:2, :], gap2[0], up_sb[:, 0:2, second], ALU.mult)
         for t in range(PACK):
             lesser(t)
 
-        w2_codes = keep.tile([P, N], U32, name="w2_codes", align_bytes=64)
+        w2_codes = keep.tile([P, N], U32, name="w2_codes", tag="far", align_bytes=64)
         w2_sc = keep.tile([P, N], U8, name="w2_sc", align_bytes=64)
         for u in range(2):
             nc.vector.quantize_mx(out=w2_codes[:, halves[u]].bitcast(FP8X4), scales=w2_sc[:, halves[u]], in_=w2_bf[u][:].rearrange("p n t -> p (n t)"))
@@ -188,7 +199,7 @@ def tile_picked_cmpex_none_p_kernel(tc, x_words, x_scales, w1, up, w2, offs, mat
 
         def share(c):
             cols = slice(P * c, P * c + P)
-            nc.vector.tensor_tensor(part[:, 2:4, cols], gap2[:, 2:4, cols], up_sb[:, 2:4, HALF + P * c : HALF + P * c + P], ALU.mult)
+            nc.vector.tensor_tensor(part[:, 2:4, cols], gap2[1][:, :, cols], up_sb[:, 2:4, HALF + P * c : HALF + P * c + P], ALU.mult)
 
         def mix(c):
             cols = slice(P * c, P * c + P)

@@ -32,7 +32,7 @@ def tile_picked_cmpex_none_p_kernel(tc, x_words, x_scales, w1, up, w2, offs, mat
         nc.sync.dma_start(offs_sb[:], offs)
         scale_table = keep.tile([P, T], U8, name="scale_table", align_bytes=64)
         nc.vector.memset(scale_table[:].bitcast(I32), 0)
-        w1_raw = keep.tile([P, PACK, H], F32, name="w1_raw", tag="raw")
+        w1_raw = keep.tile([P, PACK, H], F32, name="w1_raw")
         nc.sync.dma_start(w1_raw[:], w1.rearrange("(p j) c -> p j c", j=PACK))
         for q in range(4):
             nc.sync.dma_start(scale_table[32 * q : 32 * q + 4, :].bitcast(I32), x_scales[0, 4 * q : 4 * q + 4, :].bitcast(I32))
@@ -56,11 +56,13 @@ def tile_picked_cmpex_none_p_kernel(tc, x_words, x_scales, w1, up, w2, offs, mat
         w2_rows = w2.rearrange("(p t) n -> p t n", t=PACK)
         w2_early = keep.tile([P, PACK, HALF], F32, name="w2_early")
         nc.sync.dma_start(w2_early[:], w2_rows[:, :, halves[0]])
-        late = keep.tile([P, PACK * (S + HALF)], F32, name="late", tag="raw")
-        up_sb = late[:, 0 : PACK * S].rearrange("p (t s) -> p t s", t=PACK)
-        w2_raw = [w2_early[:], late[:, PACK * S :].rearrange("p (t n) -> p t n", t=PACK)]
-        nc.sync.dma_start(up_sb, up.rearrange("(p t) s -> p t s", t=PACK))
-        nc.sync.dma_start(w2_raw[1], w2_rows[:, :, halves[1]])
+        up_tile = keep.tile([P, PACK, S], F32, name="up_tile")
+        up_sb = up_tile[:]
+        w2_late = keep.tile([P, PACK, HALF], F32, name="w2_late")
+        up_rows = up.rearrange("(p t) s -> p t s", t=PACK)
+        nc.sync.dma_start(up_sb[:, :, halves[0]], up_rows[:, :, halves[0]])
+        nc.sync.dma_start(w2_late[:], w2_rows[:, :, halves[1]])
+        nc.sync.dma_start(up_sb[:, :, halves[1]], up_rows[:, :, halves[1]])
 
         x_codes = keep.tile([P, S], U32, name="x_codes", align_bytes=64)
         for h in range(2):
@@ -73,13 +75,14 @@ def tile_picked_cmpex_none_p_kernel(tc, x_words, x_scales, w1, up, w2, offs, mat
         tables = [keep.tile([P, S], F32, name="y_table%d" % t) for t in range(PACK)]
         plains = [keep.tile([P, HALF], F32, name="plain%d" % t, tag="plain%d" % t, align_bytes=64) for t in range(PACK - 1)]
         near_last = keep.tile([P, HALF], F32, name="near_last")
-        near = keep.tile([P, PACK, HALF], F32, name="near")
-        other_first = keep.tile([P, PACK - 1, HALF], F32, name="other_first")
-        other = [other_first[:, 0, :], other_first[:, 1, :], other_first[:, 2, :], near[:, 3, :]]
-        far = keep.tile([P, PACK, HALF], F32, name="far", tag="far", align_bytes=64)
-        gap1 = keep.tile([P, PACK, HALF], F32, name="gap1")
-        gap_last = keep.tile([P, 2, HALF], F32, name="gap_last")
-        gap2 = [near[:, 1:3, :], gap_last[:]]
+        ring = keep.tile([P, PACK * HALF + P], F32, name="ring")
+        near = ring[:, 0 : PACK * HALF].rearrange("p (t s) -> p t s", t=PACK)
+        other_pair = keep.tile([P, 2, HALF], F32, name="other_pair", tag="other_pair", align_bytes=64)
+        other_third = keep.tile([P, HALF], F32, name="other_third")
+        other = [other_pair[:, 0, :], other_pair[:, 1, :], other_third[:], ring[:, PACK * HALF - P :]]
+        far = keep.tile([P, PACK, HALF], F32, name="far")
+        gap1 = [keep.tile([P, PACK, P], F32, name="gap1_%d" % c, tag="gap1_%d" % c, align_bytes=64) for c in range(2)]
+        gap2 = keep.tile([P, PACK, HALF], F32, name="gap2")
         slope = keep.tile([P, PACK, HALF], F32, name="slope")
 
         def product(b, t, piece):
@@ -96,9 +99,9 @@ def tile_picked_cmpex_none_p_kernel(tc, x_words, x_scales, w1, up, w2, offs, mat
             )
             return bank
 
-        def round_w2(u, tag):
-            w2_bf = keep.tile([P, HALF, PACK], BF16, name="w2_bf%d" % u, tag=tag, align_bytes=64)
-            nc.gpsimd.tensor_scalar(w2_bf[:], w2_raw[u].rearrange("p t n -> p n t"), 1.0, 0.0, ALU.mult, ALU.add)
+        def round_w2(raw, tag):
+            w2_bf = keep.tile([P, raw.shape[2], PACK], BF16, name="w2_bf", tag=tag, align_bytes=64)
+            nc.gpsimd.tensor_scalar(w2_bf[:], raw.rearrange("p t n -> p n t"), 1.0, 0.0, ALU.mult, ALU.add)
             return w2_bf
 
         def fetch_near(t):
@@ -115,7 +118,7 @@ def tile_picked_cmpex_none_p_kernel(tc, x_words, x_scales, w1, up, w2, offs, mat
 
         banks = [product(0, 0, first), product(1, 1, first), product(2, 0, second), product(3, 1, second), product(4, 2, slice(0, S)), product(5, 3, slice(0, S))]
         y_far = [banks[2][:], banks[3][:], banks[4][:, second], banks[5][:, second]]
-        w2_bf = [round_w2(0, "x_table")]
+        w2_bf = [round_w2(w2_early[:], "x_table")]
         nc.scalar.copy(tables[0][:, first], banks[0][:])
         nc.vector.tensor_copy(tables[1][:, first], banks[1][:])
         nc.vector.tensor_copy(plains[1][:], banks[1][:])
@@ -131,7 +134,7 @@ def tile_picked_cmpex_none_p_kernel(tc, x_words, x_scales, w1, up, w2, offs, mat
         nc.vector.tensor_copy(plains[2][:], tables[2][:, first])
         for t in (1, 2):
             fetch_near(t)
-        w2_bf.append(round_w2(1, "plain2"))
+        w2_bf.append(round_w2(w2_late[:, :, 0:P], "plain1"))
         nc.vector.tensor_tensor(near[:, 3, :], near_last[:], banks[5][:, first], ALU.subtract)
 
         sums = [psum.tile([P, PACK, P], F32, name="sum_bank", tag="bank%d" % c) for c in range(2)]
@@ -144,38 +147,33 @@ def tile_picked_cmpex_none_p_kernel(tc, x_words, x_scales, w1, up, w2, offs, mat
                 add_turned(c, t, tables[t][:, first], start=t == 0)
                 if t < PACK - 1:
                     add_turned(c, t, tables[t][:, first])
-                    add_turned(c, t, near[:, t, :])
-                else:
-                    add_turned(c, t, near_last[:])
+        for t, source in ((0, near[:, 0, :]), (3, near_last[:]), (1, near[:, 1, :]), (2, near[:, 2, :])):
+            for c in range(2):
+                add_turned(c, t, source)
 
         fetch_other(2)
-        pairs = [slice(0, 2), slice(2, 4)]
-        for planes in pairs:
-            nc.scalar.activation(gap1[:, planes, :], near[:, planes, :], ACT.Abs, scale=2.0)
-        fetch_other(3)
-        for t in range(PACK - 1):
+        for t in range(2):
             differ(t)
-        for planes in pairs:
-            nc.vector.scalar_tensor_tensor(slope[:, planes, :], up_sb[:, planes, first], 0.5, gap1[:, planes, :], ALU.subtract, ALU.mult)
-        differ(3)
-        for u, planes in enumerate(pairs):
-            nc.scalar.activation(gap2[u], far[:, planes, :], ACT.Abs)
         for c in range(2):
+            cols = slice(P * c, P * c + P)
+            nc.scalar.activation(gap1[c][:], near[:, :, cols], ACT.Abs, scale=2.0)
+            nc.vector.scalar_tensor_tensor(slope[:, :, cols], up_sb[:, :, cols], 0.5, gap1[c][:], ALU.subtract, ALU.mult)
             for t in range(PACK):
                 add_turned(c, t, slope[:, t, :], stop=t == PACK - 1)
+        nc.scalar.activation(gap2[:, 0:2, :], far[:, 0:2, :], ACT.Abs)
+        fetch_other(3)
 
-        part = gap1
-        nc.gpsimd.tensor_tensor(part[:, 0:2, :], gap2[0], up_sb[:, 0:2, second], ALU.mult)
-        for t in range(PACK):
-            lesser(t)
+        w2_bf.append(round_w2(w2_late[:, :, P:HALF], "gap1_0"))
+        part = keep.tile([P, PACK, HALF], F32, name="part", tag="gap1_1", align_bytes=64)
+        nc.gpsimd.tensor_tensor(part[:, 0:2, :], gap2[:, 0:2, :], up_sb[:, 0:2, second], ALU.mult)
+        differ(2)
+        lesser(0)
+        lesser(1)
+        differ(3)
+        lesser(2)
+        lesser(3)
 
-        w2_codes = keep.tile([P, N], U32, name="w2_codes", tag="far", align_bytes=64)
-        w2_sc = keep.tile([P, N], U8, name="w2_sc", align_bytes=64)
-        for u in range(2):
-            nc.vector.quantize_mx(out=w2_codes[:, halves[u]].bitcast(FP8X4), scales=w2_sc[:, halves[u]], in_=w2_bf[u][:].rearrange("p n t -> p (n t)"))
-
-        backs = []
-        for c, tag in enumerate(("bank6", "bank7")):
+        def round_sum(c, tag):
             turned = keep.tile([P, 2, P, 2], BF16, name="turned%d" % c)
             nc.scalar.activation(
                 turned[:].rearrange("j u (q i) e -> j (u q) e i", i=4),
@@ -187,23 +185,35 @@ def tile_picked_cmpex_none_p_kernel(tc, x_words, x_scales, w1, up, w2, offs, mat
             back = psum.tile([P, 2, P], F32, name="back_bank", tag=tag)
             for u in range(2):
                 nc.tensor.transpose(back[:, u, :], words[:, u, :], ident[:])
-            backs.append(back)
-        z_first = []
-        for c in range(2):
+            return back
+
+        def lay_out(c, back):
             z_bf = keep.tile([P, P, PACK], BF16, name="z_first%d" % c, align_bytes=64)
             nc.scalar.copy(
                 z_bf[:].rearrange("p n t -> p (n t)").bitcast(F32).rearrange("p (q i u) -> p q u i", i=4, u=2),
-                backs[c][:].rearrange("p u (q i) -> p q u i", i=4),
+                back[:].rearrange("p u (q i) -> p q u i", i=4),
             )
-            z_first.append(z_bf)
+            return z_bf
+
+        backs = [round_sum(0, "bank6"), round_sum(1, "bank7")]
+        z_first = [lay_out(0, backs[0])]
+        nc.scalar.activation(gap2[:, 2:4, :], far[:, 2:4, :], ACT.Abs)
+        z_first.append(lay_out(1, backs[1]))
+
+        w2_codes = keep.tile([P, N], U32, name="w2_codes", tag="other_pair", align_bytes=64)
+        w2_sc = keep.tile([P, N], U8, name="w2_sc", align_bytes=64)
+
+        def quantise_w2(u):
+            cols = (first, slice(HALF, HALF + P), slice(HALF + P, N))[u]
+            nc.vector.quantize_mx(out=w2_codes[:, cols].bitcast(FP8X4), scales=w2_sc[:, cols], in_=w2_bf[u][:].rearrange("p n t -> p (n t)"))
 
         def share(c):
             cols = slice(P * c, P * c + P)
-            nc.vector.tensor_tensor(part[:, 2:4, cols], gap2[1][:, :, cols], up_sb[:, 2:4, HALF + P * c : HALF + P * c + P], ALU.mult)
+            nc.vector.tensor_tensor(part[:, 2:4, cols], gap2[:, 2:4, cols], up_sb[:, 2:4, HALF + P * c : HALF + P * c + P], ALU.mult)
 
-        def mix(c):
-            cols = slice(P * c, P * c + P)
-            z_bf = keep.tile([P, P, PACK], BF16, name="z_bf%d" % c, align_bytes=64)
+        def mix(c0, n):
+            cols = slice(c0, c0 + n)
+            z_bf = keep.tile([P, n, PACK], BF16, name="z_bf%d" % c0, align_bytes=64)
             nc.vector.tensor_tensor(
                 z_bf[:].rearrange("p (c i) t -> p c t i", i=2),
                 lo[:, :, cols].rearrange("p t (c i) -> p c t i", i=2),
@@ -212,24 +222,36 @@ def tile_picked_cmpex_none_p_kernel(tc, x_words, x_scales, w1, up, w2, offs, mat
             )
             return z_bf
 
-        def finish(c0, n, z_bf, banks):
-            last = c0 + n == S
+        def quantise_z(c0, n, z_bf):
             codes = keep.tile([P, n], U32, name="z_codes%d" % c0, align_bytes=64)
             sc = keep.tile([P, n], U8, name="z_sc%d" % c0, align_bytes=64)
             nc.vector.quantize_mx(out=codes[:].bitcast(FP8X4), scales=sc[:], in_=z_bf[:].rearrange("p n t -> p (n t)"))
+            return codes, sc
+
+        def multiply(bank, b, piece, z_mx):
+            codes, sc = z_mx
+            for e in range(2):
+                cols = slice(P * (2 * b + e), P * (2 * b + e) + P)
+                nc.tensor.matmul_mx(
+                    out=bank[:, e, piece],
+                    lhsT=w2_codes[:, cols].bitcast(FP8X4),
+                    lhsT_scale=w2_sc[:, cols],
+                    rhs=codes[:].bitcast(FP8X4),
+                    rhs_scale=sc[:],
+                    start=True,
+                    stop=True,
+                )
+
+        def finish(c0, n, z_pieces, banks):
+            last = c0 + n == S
+            width = n // len(z_pieces)
+            tiles = [psum.tile([P, 2, n], F32, name="o_bank", tag="bank%d" % banks[b]) for b in range(2)]
+            for i, z_mx in enumerate(z_pieces[:-1]):
+                for b in range(2):
+                    multiply(tiles[b], b, slice(width * i, width * (i + 1)), z_mx)
             for b in range(2):
-                bank = psum.tile([P, 2, n], F32, name="o_bank", tag="bank%d" % banks[b])
-                for e in range(2):
-                    cols = slice(P * (2 * b + e), P * (2 * b + e) + P)
-                    nc.tensor.matmul_mx(
-                        out=bank[:, e, :],
-                        lhsT=w2_codes[:, cols].bitcast(FP8X4),
-                        lhsT_scale=w2_sc[:, cols],
-                        rhs=codes[:].bitcast(FP8X4),
-                        rhs_scale=sc[:],
-                        start=True,
-                        stop=True,
-                    )
+                bank = tiles[b]
+                multiply(bank, b, slice(n - width, n), z_pieces[-1])
                 res = keep.tile([P, 2, n], F32, name="res%d_%d" % (c0, b))
                 if last and b == 1:
                     nc.vector.tensor_copy(res[:], bank[:])
@@ -238,11 +260,14 @@ def tile_picked_cmpex_none_p_kernel(tc, x_words, x_scales, w1, up, w2, offs, mat
                 queue = nc.scalar if last and b == 0 else nc.sync
                 queue.dma_start(out[2 * P * b : 2 * P * (b + 1), c0 : c0 + n].rearrange("(e p) s -> p e s", p=P), res[:])
 
+        quantise_w2(0)
+        z_mx = quantise_z(0, P, z_first[0])
+        quantise_w2(1)
+        quantise_w2(2)
+        finish(0, P, [z_mx], (2, 3))
         share(0)
-        finish(0, P, z_first[0], (2, 3))
-        z1 = mix(0)
-        finish(P, P, z_first[1], (4, 5))
+        z1 = mix(0, P)
+        finish(P, P, [quantise_z(P, P, z_first[1])], (4, 5))
         share(1)
-        finish(HALF, P, z1, (0, 1))
-        z2 = mix(1)
-        finish(HALF + P, P, z2, (6, 7))
+        finish(HALF, P, [quantise_z(HALF, P, z1)], (0, 1))
+        finish(HALF + P, P, [quantise_z(HALF + P, P, mix(P, P))], (6, 7))

@@ -163,8 +163,7 @@ def tile_picked_cmpex_none_p_kernel(tc, x_words, x_scales, w1, up, w2, offs, mat
         nc.scalar.activation(gap2[:, 0:2, :], far[:, 0:2, :], ACT.Abs)
         fetch_other(3)
 
-        w2_bf.append(round_w2(w2_late[:, :, P:HALF], "gap1_0"))
-        part = keep.tile([P, PACK, HALF], F32, name="part", tag="gap1_1", align_bytes=64)
+        part = keep.tile([P, PACK, HALF], F32, name="part", tag="gap1_0", align_bytes=64)
         nc.gpsimd.tensor_tensor(part[:, 0:2, :], gap2[:, 0:2, :], up_sb[:, 0:2, second], ALU.mult)
         differ(2)
         lesser(0)
@@ -174,7 +173,7 @@ def tile_picked_cmpex_none_p_kernel(tc, x_words, x_scales, w1, up, w2, offs, mat
         lesser(3)
 
         def round_sum(c, tag):
-            turned = keep.tile([P, 2, P, 2], BF16, name="turned%d" % c)
+            turned = keep.tile([P, 2, P, 2], BF16, name="turned%d" % c, tag="turned%d" % c, align_bytes=64)
             nc.scalar.activation(
                 turned[:].rearrange("j u (q i) e -> j (u q) e i", i=4),
                 sums[c][:].rearrange("j (e u) (q i) -> j (u q) e i", e=2, i=4),
@@ -199,6 +198,8 @@ def tile_picked_cmpex_none_p_kernel(tc, x_words, x_scales, w1, up, w2, offs, mat
         z_first = [lay_out(0, backs[0])]
         nc.scalar.activation(gap2[:, 2:4, :], far[:, 2:4, :], ACT.Abs)
         z_first.append(lay_out(1, backs[1]))
+        w2_bf.append(keep.tile([P, P, PACK], BF16, name="w2_last", tag="turned1", align_bytes=64))
+        nc.scalar.copy(w2_bf[2][:].rearrange("p (c i) t -> p c t i", i=4), w2_late[:, :, P:HALF].rearrange("p t (c i) -> p c t i", i=4))
 
         w2_codes = keep.tile([P, N], U32, name="w2_codes", tag="other_pair", align_bytes=64)
         w2_sc = keep.tile([P, N], U8, name="w2_sc", align_bytes=64)
@@ -261,12 +262,12 @@ def tile_picked_cmpex_none_p_kernel(tc, x_words, x_scales, w1, up, w2, offs, mat
                 queue.dma_start(out[2 * P * b : 2 * P * (b + 1), c0 : c0 + n].rearrange("(e p) s -> p e s", p=P), res[:])
 
         quantise_w2(0)
-        z_mx = quantise_z(0, P, z_first[0])
         quantise_w2(1)
+        share(0)
+        z_mx = quantise_z(0, P, z_first[0])
+        z1 = mix(0, P)
         quantise_w2(2)
         finish(0, P, [z_mx], (2, 3))
-        share(0)
-        z1 = mix(0, P)
         finish(P, P, [quantise_z(P, P, z_first[1])], (4, 5))
         share(1)
         finish(HALF, P, [quantise_z(HALF, P, z1)], (0, 1))

@@ -80,7 +80,7 @@ def tile_picked_cmpex_none_p_kernel(tc, x_words, x_scales, w1, up, w2, offs, mat
         other_pair = keep.tile([P, 2, HALF], F32, name="other_pair", tag="other_pair", align_bytes=64)
         other_third = keep.tile([P, HALF], F32, name="other_third")
         other = [other_pair[:, 0, :], other_pair[:, 1, :], other_third[:], ring[:, PACK * HALF - P :]]
-        far = keep.tile([P, PACK, HALF], F32, name="far")
+        far = keep.tile([P, PACK, HALF], F32, name="far", align_bytes=64)
         gap1 = [keep.tile([P, PACK, P], F32, name="gap1_%d" % c, tag="gap1_%d" % c, align_bytes=64) for c in range(2)]
         gap2 = keep.tile([P, PACK, HALF], F32, name="gap2")
         slope = keep.tile([P, PACK, HALF], F32, name="slope")
@@ -172,15 +172,14 @@ def tile_picked_cmpex_none_p_kernel(tc, x_words, x_scales, w1, up, w2, offs, mat
         lesser(2)
         lesser(3)
 
-        def round_sum(c, tag):
-            turned = keep.tile([P, 2, P, 2], BF16, name="turned%d" % c, tag="turned%d" % c, align_bytes=64)
+        def round_sum(c, turned, tag):
             nc.scalar.activation(
-                turned[:].rearrange("j u (q i) e -> j (u q) e i", i=4),
+                turned.rearrange("j u (q i) e -> j (u q) e i", i=4),
                 sums[c][:].rearrange("j (e u) (q i) -> j (u q) e i", e=2, i=4),
                 ACT.Copy,
                 scale=0.5,
             )
-            words = turned[:].rearrange("j u p e -> j u (p e)").bitcast(F32)
+            words = turned.rearrange("j u p e -> j u (p e)").bitcast(F32)
             back = psum.tile([P, 2, P], F32, name="back_bank", tag=tag)
             for u in range(2):
                 nc.tensor.transpose(back[:, u, :], words[:, u, :], ident[:])
@@ -194,10 +193,13 @@ def tile_picked_cmpex_none_p_kernel(tc, x_words, x_scales, w1, up, w2, offs, mat
             )
             return z_bf
 
-        backs = [round_sum(0, "bank6"), round_sum(1, "bank7")]
-        z_first = [lay_out(0, backs[0])]
-        nc.scalar.activation(gap2[:, 2:4, :], far[:, 2:4, :], ACT.Abs)
-        z_first.append(lay_out(1, backs[1]))
+        nc.scalar.activation(gap2[:, 2, :], far[:, 2, :], ACT.Abs)
+        nc.gpsimd.tensor_tensor(part[:, 2, :], gap2[:, 2, :], up_sb[:, 2, second], ALU.mult)
+        backs = [round_sum(0, far[:, 2, :].bitcast(BF16).rearrange("j (u p e) -> j u p e", u=2, e=2), "bank6")]
+        nc.scalar.activation(gap2[:, 3, :], far[:, 3, :], ACT.Abs)
+        turned = keep.tile([P, 2, P, 2], BF16, name="turned", tag="turned1", align_bytes=64)
+        backs.append(round_sum(1, turned[:], "bank7"))
+        z_first = [lay_out(c, backs[c]) for c in range(2)]
         w2_bf.append(keep.tile([P, P, PACK], BF16, name="w2_last", tag="turned1", align_bytes=64))
         nc.scalar.copy(w2_bf[2][:].rearrange("p (c i) t -> p c t i", i=4), w2_late[:, :, P:HALF].rearrange("p t (c i) -> p c t i", i=4))
 
@@ -210,7 +212,7 @@ def tile_picked_cmpex_none_p_kernel(tc, x_words, x_scales, w1, up, w2, offs, mat
 
         def share(c):
             cols = slice(P * c, P * c + P)
-            nc.vector.tensor_tensor(part[:, 2:4, cols], gap2[:, 2:4, cols], up_sb[:, 2:4, HALF + P * c : HALF + P * c + P], ALU.mult)
+            nc.vector.tensor_tensor(part[:, 3, cols], gap2[:, 3, cols], up_sb[:, 3, HALF + P * c : HALF + P * c + P], ALU.mult)
 
         def mix(c0, n):
             cols = slice(c0, c0 + n)

@@ -195,20 +195,22 @@ def tile_picked_cmpex_none_p_kernel(tc, x_words, x_scales, w1, up, w2, offs, mat
 
         nc.scalar.activation(gap2[:, 2, :], far[:, 2, :], ACT.Abs)
         nc.gpsimd.tensor_tensor(part[:, 2, :], gap2[:, 2, :], up_sb[:, 2, second], ALU.mult)
-        backs = [round_sum(0, far[:, 2, :].bitcast(BF16).rearrange("j (u p e) -> j u p e", u=2, e=2), "bank6")]
+        freed = far[:, 2, :].bitcast(BF16)
+        backs = [round_sum(0, freed.rearrange("j (u p e) -> j u p e", u=2, e=2), "bank6")]
         nc.scalar.activation(gap2[:, 3, :], far[:, 3, :], ACT.Abs)
         turned = keep.tile([P, 2, P, 2], BF16, name="turned", tag="turned1", align_bytes=64)
         backs.append(round_sum(1, turned[:], "bank7"))
-        z_first = [lay_out(c, backs[c]) for c in range(2)]
-        w2_bf.append(keep.tile([P, P, PACK], BF16, name="w2_last", tag="turned1", align_bytes=64))
-        nc.scalar.copy(w2_bf[2][:].rearrange("p (c i) t -> p c t i", i=4), w2_late[:, :, P:HALF].rearrange("p t (c i) -> p c t i", i=4))
+        z_first = [lay_out(0, backs[0])]
+        w2_bf.append(freed.rearrange("p (n t) -> p n t", t=PACK))
+        nc.scalar.copy(w2_bf[2].rearrange("p (c i) t -> p c t i", i=4), w2_late[:, :, P:HALF].rearrange("p t (c i) -> p c t i", i=4))
+        z_first.append(lay_out(1, backs[1]))
 
         w2_codes = keep.tile([P, N], U32, name="w2_codes", tag="other_pair", align_bytes=64)
         w2_sc = keep.tile([P, N], U8, name="w2_sc", align_bytes=64)
 
         def quantise_w2(u):
             cols = (first, slice(HALF, HALF + P), slice(HALF + P, N))[u]
-            nc.vector.quantize_mx(out=w2_codes[:, cols].bitcast(FP8X4), scales=w2_sc[:, cols], in_=w2_bf[u][:].rearrange("p n t -> p (n t)"))
+            nc.vector.quantize_mx(out=w2_codes[:, cols].bitcast(FP8X4), scales=w2_sc[:, cols], in_=w2_bf[u][:, :, :].rearrange("p n t -> p (n t)"))
 
         def share(c):
             cols = slice(P * c, P * c + P)
@@ -266,11 +268,11 @@ def tile_picked_cmpex_none_p_kernel(tc, x_words, x_scales, w1, up, w2, offs, mat
         quantise_w2(0)
         quantise_w2(1)
         share(0)
+        share(1)
         z_mx = quantise_z(0, P, z_first[0])
         z1 = mix(0, P)
         quantise_w2(2)
         finish(0, P, [z_mx], (2, 3))
         finish(P, P, [quantise_z(P, P, z_first[1])], (4, 5))
-        share(1)
         finish(HALF, P, [quantise_z(HALF, P, z1)], (0, 1))
         finish(HALF + P, P, [quantise_z(HALF + P, P, mix(P, P))], (6, 7))

@@ -26,16 +26,18 @@ def tile_picked_cmpex_none_p_kernel(tc, x_words, x_scales, w1, up, w2, offs, mat
     halves = [slice(0, HALF), slice(HALF, S)]
     with ExitStack() as ctx:
         keep = ctx.enter_context(tc.tile_pool(name="keep", bufs=1))
+        shared = ctx.enter_context(tc.tile_pool(name="shared", bufs=1))
         psum = ctx.enter_context(tc.psum_pool(name="psum", bufs=1))
 
         offs_sb = keep.tile([P, S // 16], U16, name="offs_sb")
         nc.sync.dma_start(offs_sb[:], offs)
-        scale_table = keep.tile([P, T], U8, name="scale_table", align_bytes=64)
+        scale_table = shared.tile([P, T], U8, name="scale_table", offset=4 * PACK * N - T // 2, align_bytes=64)
         nc.vector.memset(scale_table[:].bitcast(I32), 0)
         w1_raw = keep.tile([P, PACK, H], F32, name="w1_raw")
-        nc.sync.dma_start(w1_raw[:], w1.rearrange("(p j) c -> p j c", j=PACK))
-        for q in range(4):
-            nc.sync.dma_start(scale_table[32 * q : 32 * q + 4, :].bitcast(I32), x_scales[0, 4 * q : 4 * q + 4, :].bitcast(I32))
+        w1_rows = w1.rearrange("(p j) c -> p j c", j=PACK)
+        nc.sync.dma_start(w1_raw[:, 0:2, :], w1_rows[:, 0:2, :])
+        nc.sync.dma_start(scale_table[0:P:8, :].bitcast(I32), x_scales[0].bitcast(I32))
+        nc.sync.dma_start(w1_raw[:, 2:4, :], w1_rows[:, 2:4, :])
         x_table = keep.tile([P, T], U32, name="x_table", tag="x_table", align_bytes=64)
         nc.sync.dma_start(x_table[:].bitcast(I32), x_words[0].rearrange("p n t -> p (n t)").bitcast(I32))
         mate_sb = keep.tile([P, S // 16], U16, name="mate_sb")
@@ -45,23 +47,27 @@ def tile_picked_cmpex_none_p_kernel(tc, x_words, x_scales, w1, up, w2, offs, mat
         w1_codes = [keep.tile([P, 2 * P], U32, name="w1_codes%d" % u, align_bytes=64) for u in range(2)]
         w1_sc = [keep.tile([P, 2 * P], U8, name="w1_sc%d" % u, align_bytes=64) for u in range(2)]
         w1_cols = w1_raw[:].rearrange("p j (m t) -> p m j t", t=PACK)
-        nc.vector.tensor_copy(w1_bf[0][:, :, 0 : P // 2, :].rearrange("p e m j -> p m j e"), w1_cols[:, 0 : P // 2, :, 0:2])
-        nc.scalar.copy(w1_bf[1][:].rearrange("p e m j -> p m j e"), w1_cols[:, :, :, 2:4])
-        nc.scalar.copy(w1_bf[0][:, :, P // 2 : P, :].rearrange("p e m j -> p m j e"), w1_cols[:, P // 2 : P, :, 0:2])
         x_sc = keep.tile([P, S], U8, name="x_sc", align_bytes=64)
-        nc.vector.tensor_copy(x_sc[:], scale_table[:].indirect(offs_sb[:]))
-        for u in (1, 0):
+        nc.vector.memset(x_sc[:].bitcast(I32), 0)
+        picked_sc = keep.tile([P, S], U8, name="picked_sc", align_bytes=64)
+        nc.vector.tensor_copy(picked_sc[:], scale_table[:].indirect(offs_sb[:]))
+        for q in range(4):
+            nc.sync.dma_start(x_sc[32 * q : 32 * q + 4, :].bitcast(I32), picked_sc[32 * q : 32 * q + 32 : 8, :].bitcast(I32))
+        nc.vector.tensor_copy(w1_bf[0][:].rearrange("p e m j -> p m j e"), w1_cols[:, :, :, 0:2])
+        for j in (0, 2):
+            nc.scalar.copy(w1_bf[1][:, :, :, j : j + 2].rearrange("p e m j -> p m j e"), w1_cols[:, :, j : j + 2, 2:4])
+        for u in (0, 1):
             nc.vector.quantize_mx(out=w1_codes[u][:].bitcast(FP8X4), scales=w1_sc[u][:], in_=w1_bf[u][:].rearrange("p e m j -> p (e m j)"))
 
         w2_rows = w2.rearrange("(p t) n -> p t n", t=PACK)
-        w2_early = keep.tile([P, PACK, HALF], F32, name="w2_early")
-        nc.sync.dma_start(w2_early[:], w2_rows[:, :, halves[0]])
-        up_tile = keep.tile([P, PACK, S], F32, name="up_tile")
+        w2_raw = shared.tile([P, 2, PACK, HALF], F32, name="w2_raw", offset=0)
+        w2_early, w2_late = w2_raw[:, 0, :, :], w2_raw[:, 1, :, :]
+        nc.sync.dma_start(w2_early, w2_rows[:, :, halves[0]])
+        up_tile = shared.tile([P, PACK, S], F32, name="up_tile", offset=4 * PACK * N)
         up_sb = up_tile[:]
-        w2_late = keep.tile([P, PACK, HALF], F32, name="w2_late")
         up_rows = up.rearrange("(p t) s -> p t s", t=PACK)
         nc.sync.dma_start(up_sb[:, :, halves[0]], up_rows[:, :, halves[0]])
-        nc.sync.dma_start(w2_late[:], w2_rows[:, :, halves[1]])
+        nc.sync.dma_start(w2_late, w2_rows[:, :, halves[1]])
         nc.sync.dma_start(up_sb[:, :, halves[1]], up_rows[:, :, halves[1]])
 
         x_codes = keep.tile([P, S], U32, name="x_codes", align_bytes=64)
@@ -118,7 +124,7 @@ def tile_picked_cmpex_none_p_kernel(tc, x_words, x_scales, w1, up, w2, offs, mat
 
         banks = [product(0, 0, first), product(1, 1, first), product(2, 0, second), product(3, 1, second), product(4, 2, slice(0, S)), product(5, 3, slice(0, S))]
         y_far = [banks[2][:], banks[3][:], banks[4][:, second], banks[5][:, second]]
-        w2_bf = [round_w2(w2_early[:], "x_table")]
+        w2_bf = [round_w2(w2_early, "x_table")]
         nc.scalar.copy(tables[0][:, first], banks[0][:])
         nc.vector.tensor_copy(tables[1][:, first], banks[1][:])
         nc.vector.tensor_copy(plains[1][:], banks[1][:])

@@ -30,12 +30,12 @@ def tile_picked_cmpex_none_p_kernel(tc, x_words, x_scales, w1, up, w2, offs, mat
         psum = ctx.enter_context(tc.psum_pool(name="psum", bufs=1))
 
         offs_sb = keep.tile([P, S // 16], U16, name="offs_sb")
-        nc.sync.dma_start(offs_sb[:], offs)
         scale_table = shared.tile([P, T], U8, name="scale_table", offset=4 * PACK * N - T // 2, align_bytes=64)
         nc.vector.memset(scale_table[:].bitcast(I32), 0)
         w1_raw = keep.tile([P, PACK, H], F32, name="w1_raw")
         w1_rows = w1.rearrange("(p j) c -> p j c", j=PACK)
         nc.sync.dma_start(w1_raw[:, 0:2, :], w1_rows[:, 0:2, :])
+        nc.sync.dma_start(offs_sb[:], offs)
         nc.sync.dma_start(scale_table[0:P:8, :].bitcast(I32), x_scales[0].bitcast(I32))
         nc.sync.dma_start(w1_raw[:, 2:4, :], w1_rows[:, 2:4, :])
         x_table = keep.tile([P, T], U32, name="x_table", tag="x_table", align_bytes=64)
@@ -180,8 +180,8 @@ def tile_picked_cmpex_none_p_kernel(tc, x_words, x_scales, w1, up, w2, offs, mat
 
         def round_sum(c, turned, tag):
             nc.scalar.activation(
-                turned.rearrange("j u (q i) e -> j (u q) e i", i=4),
-                sums[c][:].rearrange("j (e u) (q i) -> j (u q) e i", e=2, i=4),
+                turned,
+                sums[c][:].rearrange("j (e u) p -> j u p e", e=2),
                 ACT.Copy,
                 scale=0.5,
             )
@@ -194,8 +194,8 @@ def tile_picked_cmpex_none_p_kernel(tc, x_words, x_scales, w1, up, w2, offs, mat
         def lay_out(c, back):
             z_bf = keep.tile([P, P, PACK], BF16, name="z_first%d" % c, align_bytes=64)
             nc.scalar.copy(
-                z_bf[:].rearrange("p n t -> p (n t)").bitcast(F32).rearrange("p (q i u) -> p q u i", i=4, u=2),
-                back[:].rearrange("p u (q i) -> p q u i", i=4),
+                z_bf[:].rearrange("p n t -> p (n t)").bitcast(F32).rearrange("p (n u) -> p n u", u=2),
+                back[:].rearrange("p u n -> p n u"),
             )
             return z_bf
 

@@ -226,9 +226,9 @@ def tile_picked_cmpex_none_p_kernel(tc, x_words, x_scales, w1, up, w2, offs, mat
             cols = slice(c0, c0 + n)
             z_bf = keep.tile([P, n, PACK], BF16, name="z_bf%d" % c0, align_bytes=64)
             nc.vector.tensor_tensor(
-                z_bf[:].rearrange("p (c i) t -> p c t i", i=2),
-                lo[:, :, cols].rearrange("p t (c i) -> p c t i", i=2),
-                part[:, :, cols].rearrange("p t (c i) -> p c t i", i=2),
+                z_bf[:].rearrange("p (c i) t -> p c t i", i=4),
+                lo[:, :, cols].rearrange("p t (c i) -> p c t i", i=4),
+                part[:, :, cols].rearrange("p t (c i) -> p c t i", i=4),
                 ALU.add,
             )
             return z_bf

@@ -19,6 +19,7 @@ ACT = mybir.ActivationFunctionType
 P = 128
 PACK = 4
 HALF = S // 2
+LEAD = 3 * H // 2
 
 
 def tile_picked_cmpex_none_p_kernel(tc, x_words, x_scales, w1, up, w2, offs, mate, out):
@@ -33,11 +34,12 @@ def tile_picked_cmpex_none_p_kernel(tc, x_words, x_scales, w1, up, w2, offs, mat
         scale_table = shared.tile([P, T], U8, name="scale_table", offset=4 * PACK * N - T // 2, align_bytes=64)
         nc.vector.memset(scale_table[:].bitcast(I32), 0)
         w1_raw = keep.tile([P, PACK, H], F32, name="w1_raw")
-        w1_rows = w1.rearrange("(p j) c -> p j c", j=PACK)
-        nc.sync.dma_start(w1_raw[:, 0:2, :], w1_rows[:, 0:2, :])
+        w1_rows = w1.rearrange("(p j) c -> p (j c)", j=PACK)
+        w1_flat = w1_raw[:].rearrange("p j c -> p (j c)")
+        nc.sync.dma_start(w1_flat[:, 0:LEAD], w1_rows[:, 0:LEAD])
         nc.sync.dma_start(offs_sb[:], offs)
         nc.sync.dma_start(scale_table[0:P:8, :].bitcast(I32), x_scales[0].bitcast(I32))
-        nc.sync.dma_start(w1_raw[:, 2:4, :], w1_rows[:, 2:4, :])
+        nc.sync.dma_start(w1_flat[:, LEAD:], w1_rows[:, LEAD:])
         x_table = keep.tile([P, T], U32, name="x_table", tag="x_table", align_bytes=64)
         nc.sync.dma_start(x_table[:].bitcast(I32), x_words[0].rearrange("p n t -> p (n t)").bitcast(I32))
         mate_sb = keep.tile([P, S // 16], U16, name="mate_sb")
@@ -54,7 +56,7 @@ def tile_picked_cmpex_none_p_kernel(tc, x_words, x_scales, w1, up, w2, offs, mat
         for q in range(4):
             nc.sync.dma_start(x_sc[32 * q : 32 * q + 4, :].bitcast(I32), picked_sc[32 * q : 32 * q + 32 : 8, :].bitcast(I32))
         nc.vector.tensor_copy(w1_bf[0][:].rearrange("p e m j -> p m j e"), w1_cols[:, :, :, 0:2])
-        for j in (0, 2):
+        for j in (2, 0):
             nc.scalar.copy(w1_bf[1][:, :, :, j : j + 2].rearrange("p e m j -> p m j e"), w1_cols[:, :, j : j + 2, 2:4])
         for u in (0, 1):
             nc.vector.quantize_mx(out=w1_codes[u][:].bitcast(FP8X4), scales=w1_sc[u][:], in_=w1_bf[u][:].rearrange("p e m j -> p (e m j)"))

from contextlib import ExitStack

import concourse.mybir as mybir
from concourse.masks import make_identity

K, T, S, N, H = 512, 2048, 512, 512, 512
FLOPS = 2 * K * H * S + 2 * H * N * S

F32 = mybir.dt.float32
BF16 = mybir.dt.bfloat16
I32 = mybir.dt.int32
U32 = mybir.dt.uint32
U16 = mybir.dt.uint16
U8 = mybir.dt.uint8
FP8X4 = mybir.dt.float8_e4m3fn_x4
ALU = mybir.AluOpType
ACT = mybir.ActivationFunctionType

P = 128
PACK = 4
HALF = S // 2
LEAD = 3 * H // 2


def tile_picked_cmpex_none_p_kernel(tc, x_words, x_scales, w1, up, w2, offs, mate, out):
    nc = tc.nc
    halves = [slice(0, HALF), slice(HALF, S)]
    with ExitStack() as ctx:
        keep = ctx.enter_context(tc.tile_pool(name="keep", bufs=1))
        shared = ctx.enter_context(tc.tile_pool(name="shared", bufs=1))
        psum = ctx.enter_context(tc.psum_pool(name="psum", bufs=1))

        offs_sb = keep.tile([P, S // 16], U16, name="offs_sb")
        scale_table = shared.tile([P, T], U8, name="scale_table", offset=4 * PACK * N - T // 2, align_bytes=64)
        nc.vector.memset(scale_table[:].bitcast(I32), 0)
        w1_raw = keep.tile([P, PACK, H], F32, name="w1_raw")
        w1_rows = w1.rearrange("(p j) c -> p (j c)", j=PACK)
        w1_flat = w1_raw[:].rearrange("p j c -> p (j c)")
        nc.sync.dma_start(w1_flat[:, 0:LEAD], w1_rows[:, 0:LEAD])
        nc.sync.dma_start(offs_sb[:], offs)
        nc.sync.dma_start(scale_table[0:P:8, :].bitcast(I32), x_scales[0].bitcast(I32))
        nc.sync.dma_start(w1_flat[:, LEAD:], w1_rows[:, LEAD:])
        x_table = keep.tile([P, T], U32, name="x_table", tag="x_table", align_bytes=64)
        nc.sync.dma_start(x_table[:].bitcast(I32), x_words[0].rearrange("p n t -> p (n t)").bitcast(I32))
        mate_sb = keep.tile([P, S // 16], U16, name="mate_sb")
        nc.sync.dma_start(mate_sb[:], mate)

        w1_bf = [keep.tile([P, 2, P, PACK], BF16, name="w1_bf%d" % u, align_bytes=64) for u in range(2)]
        w1_codes = [keep.tile([P, 2 * P], U32, name="w1_codes%d" % u, align_bytes=64) for u in range(2)]
        w1_sc = [keep.tile([P, 2 * P], U8, name="w1_sc%d" % u, align_bytes=64) for u in range(2)]
        w1_cols = w1_raw[:].rearrange("p j (m t) -> p m j t", t=PACK)
        x_sc = keep.tile([P, S], U8, name="x_sc", align_bytes=64)
        nc.vector.memset(x_sc[:].bitcast(I32), 0)
        picked_sc = keep.tile([P, S], U8, name="picked_sc", align_bytes=64)
        nc.vector.tensor_copy(picked_sc[:], scale_table[:].indirect(offs_sb[:]))
        for q in range(4):
            nc.sync.dma_start(x_sc[32 * q : 32 * q + 4, :].bitcast(I32), picked_sc[32 * q : 32 * q + 32 : 8, :].bitcast(I32))
        nc.vector.tensor_copy(w1_bf[0][:].rearrange("p e m j -> p m j e"), w1_cols[:, :, :, 0:2])
        for j in (2, 0):
            nc.scalar.copy(w1_bf[1][:, :, :, j : j + 2].rearrange("p e m j -> p m j e"), w1_cols[:, :, j : j + 2, 2:4])
        for u in (0, 1):
            nc.vector.quantize_mx(out=w1_codes[u][:].bitcast(FP8X4), scales=w1_sc[u][:], in_=w1_bf[u][:].rearrange("p e m j -> p (e m j)"))

        w2_rows = w2.rearrange("(p t) n -> p t n", t=PACK)
        w2_raw = shared.tile([P, 2, PACK, HALF], F32, name="w2_raw", offset=0)
        w2_early, w2_late = w2_raw[:, 0, :, :], w2_raw[:, 1, :, :]
        nc.sync.dma_start(w2_early, w2_rows[:, :, halves[0]])
        up_tile = shared.tile([P, PACK, S], F32, name="up_tile", offset=4 * PACK * N)
        up_sb = up_tile[:]
        up_rows = up.rearrange("(p t) s -> p t s", t=PACK)
        nc.sync.dma_start(up_sb[:, :, halves[0]], up_rows[:, :, halves[0]])
        nc.sync.dma_start(w2_late, w2_rows[:, :, halves[1]])
        nc.sync.dma_start(up_sb[:, :, halves[1]], up_rows[:, :, halves[1]])

        x_codes = keep.tile([P, S], U32, name="x_codes", align_bytes=64)
        for h in range(2):
            nc.vector.tensor_copy(x_codes[:, halves[h]], x_table[:].indirect(offs_sb[:, 16 * h : 16 * h + 16]))

        ident = keep.tile([P, P], F32, name="ident")
        make_identity(nc, ident[:])
        first, second = halves
        lo = up_sb[:, :, first]
        tables = [keep.tile([P, S], F32, name="y_table%d" % t) for t in range(PACK)]
        plains = [keep.tile([P, HALF], F32, name="plain%d" % t, tag="plain%d" % t, align_bytes=64) for t in range(PACK - 1)]
        near_last = keep.tile([P, HALF], F32, name="near_last")
        ring = keep.tile([P, PACK * HALF + P], F32, name="ring")
        near = ring[:, 0 : PACK * HALF].rearrange("p (t s) -> p t s", t=PACK)
        other_pair = keep.tile([P, 2, HALF], F32, name="other_pair", tag="other_pair", align_bytes=64)
        other_third = keep.tile([P, HALF], F32, name="other_third")
        other = [other_pair[:, 0, :], other_pair[:, 1, :], other_third[:], ring[:, PACK * HALF - P :]]
        far = keep.tile([P, PACK, HALF], F32, name="far", align_bytes=64)
        gap1 = [keep.tile([P, PACK, P], F32, name="gap1_%d" % c, tag="gap1_%d" % c, align_bytes=64) for c in range(2)]
        gap2 = keep.tile([P, PACK, HALF], F32, name="gap2")
        slope = keep.tile([P, PACK, HALF], F32, name="slope")

        def product(b, t, piece):
            cols = slice(P * (t % 2), P * (t % 2) + P)
            bank = psum.tile([P, piece.stop - piece.start], F32, name="y_bank", tag="bank%d" % b)
            nc.tensor.matmul_mx(
                out=bank[:],
                lhsT=w1_codes[t // 2][:, cols].bitcast(FP8X4),
                lhsT_scale=w1_sc[t // 2][:, cols],
                rhs=x_codes[:, piece].bitcast(FP8X4),
                rhs_scale=x_sc[:, piece],
                start=True,
                stop=True,
            )
            return bank

        def round_w2(raw, tag):
            w2_bf = keep.tile([P, raw.shape[2], PACK], BF16, name="w2_bf", tag=tag, align_bytes=64)
            nc.gpsimd.tensor_scalar(w2_bf[:], raw.rearrange("p t n -> p n t"), 1.0, 0.0, ALU.mult, ALU.add)
            return w2_bf

        def fetch_near(t):
            nc.vector.tensor_tensor(near[:, t, :], tables[t][:].indirect(mate_sb[:, 0:16]), plains[t][:], ALU.subtract)

        def fetch_other(t):
            nc.scalar.activation(other[t], tables[t][:].indirect(mate_sb[:, 16:32]), ACT.Copy)

        def differ(t):
            nc.vector.tensor_tensor(far[:, t, :], other[t], y_far[t], ALU.subtract)

        def lesser(t):
            nc.vector.tensor_tensor(lo[:, t, :], other[t], y_far[t], ALU.min)

        banks = [product(0, 0, first), product(1, 1, first), product(2, 0, second), product(3, 1, second), product(4, 2, slice(0, S)), product(5, 3, slice(0, S))]
        y_far = [banks[2][:], banks[3][:], banks[4][:, second], banks[5][:, second]]
        w2_bf = [round_w2(w2_early, "x_table")]
        nc.scalar.copy(tables[0][:, first], banks[0][:])
        nc.vector.tensor_copy(tables[1][:, first], banks[1][:])
        nc.vector.tensor_copy(plains[1][:], banks[1][:])
        nc.scalar.copy(tables[0][:, second], banks[2][:])
        nc.vector.tensor_copy(tables[1][:, second], banks[3][:])
        nc.vector.tensor_copy(plains[0][:], banks[0][:])
        nc.vector.tensor_copy(tables[2][:], banks[4][:])
        for t in (0, 1):
            fetch_other(t)
        nc.scalar.copy(tables[3][:], banks[5][:])
        nc.scalar.activation(near_last[:], tables[3][:].indirect(mate_sb[:, 0:16]), ACT.Copy)
        fetch_near(0)
        nc.vector.tensor_copy(plains[2][:], tables[2][:, first])
        for t in (1, 2):
            fetch_near(t)
        w2_bf.append(round_w2(w2_late[:, :, 0:P], "plain1"))
        nc.vector.tensor_tensor(near[:, 3, :], near_last[:], banks[5][:, first], ALU.subtract)

        sums = [psum.tile([P, PACK, P], F32, name="sum_bank", tag="bank%d" % c) for c in range(2)]

        def add_turned(c, t, source, start=False, stop=False):
            nc.tensor.matmul(sums[c][:, 2 * (t % 2) + t // 2, :], source[:, P * c : P * c + P], ident[:], is_transpose=True, start=start, stop=stop)

        for t in range(PACK):
            for c in range(2):
                add_turned(c, t, tables[t][:, first], start=t == 0)
                if t < PACK - 1:
                    add_turned(c, t, tables[t][:, first])
        for t, source in ((0, near[:, 0, :]), (3, near_last[:]), (1, near[:, 1, :]), (2, near[:, 2, :])):
            for c in range(2):
                add_turned(c, t, source)

        fetch_other(2)
        for t in range(2):
            differ(t)
        for c in range(2):
            cols = slice(P * c, P * c + P)
            nc.scalar.activation(gap1[c][:], near[:, :, cols], ACT.Abs, scale=2.0)
            nc.vector.scalar_tensor_tensor(slope[:, :, cols], up_sb[:, :, cols], 0.5, gap1[c][:], ALU.subtract, ALU.mult)
            for t in range(PACK):
                add_turned(c, t, slope[:, t, :], stop=t == PACK - 1)
        nc.scalar.activation(gap2[:, 0:2, :], far[:, 0:2, :], ACT.Abs)
        fetch_other(3)

        part = keep.tile([P, PACK, HALF], F32, name="part", tag="gap1_0", align_bytes=64)
        nc.gpsimd.tensor_tensor(part[:, 0:2, :], gap2[:, 0:2, :], up_sb[:, 0:2, second], ALU.mult)
        differ(2)
        lesser(0)
        lesser(1)
        differ(3)
        lesser(2)
        lesser(3)

        def round_sum(c, turned, tag):
            nc.scalar.activation(
                turned,
                sums[c][:].rearrange("j (e u) p -> j u p e", e=2),
                ACT.Copy,
                scale=0.5,
            )
            words = turned.rearrange("j u p e -> j u (p e)").bitcast(F32)
            back = psum.tile([P, 2, P], F32, name="back_bank", tag=tag)
            for u in range(2):
                nc.tensor.transpose(back[:, u, :], words[:, u, :], ident[:])
            return back

        def lay_out(c, back):
            z_bf = keep.tile([P, P, PACK], BF16, name="z_first%d" % c, align_bytes=64)
            nc.scalar.copy(
                z_bf[:].rearrange("p n t -> p (n t)").bitcast(F32).rearrange("p (n u) -> p n u", u=2),
                back[:].rearrange("p u n -> p n u"),
            )
            return z_bf

        nc.scalar.activation(gap2[:, 2, :], far[:, 2, :], ACT.Abs)
        nc.gpsimd.tensor_tensor(part[:, 2, :], gap2[:, 2, :], up_sb[:, 2, second], ALU.mult)
        freed = far[:, 2, :].bitcast(BF16)
        backs = [round_sum(0, freed.rearrange("j (u p e) -> j u p e", u=2, e=2), "bank6")]
        nc.scalar.activation(gap2[:, 3, :], far[:, 3, :], ACT.Abs)
        turned = keep.tile([P, 2, P, 2], BF16, name="turned", tag="turned1", align_bytes=64)
        backs.append(round_sum(1, turned[:], "bank7"))
        z_first = [lay_out(0, backs[0])]
        w2_bf.append(freed.rearrange("p (n t) -> p n t", t=PACK))
        nc.scalar.copy(w2_bf[2].rearrange("p (c i) t -> p c t i", i=4), w2_late[:, :, P:HALF].rearrange("p t (c i) -> p c t i", i=4))
        z_first.append(lay_out(1, backs[1]))

        w2_codes = keep.tile([P, N], U32, name="w2_codes", tag="other_pair", align_bytes=64)
        w2_sc = keep.tile([P, N], U8, name="w2_sc", align_bytes=64)

        def quantise_w2(u):
            cols = (first, slice(HALF, HALF + P), slice(HALF + P, N))[u]
            nc.vector.quantize_mx(out=w2_codes[:, cols].bitcast(FP8X4), scales=w2_sc[:, cols], in_=w2_bf[u][:, :, :].rearrange("p n t -> p (n t)"))

        def share(c):
            cols = slice(P * c, P * c + P)
            nc.vector.tensor_tensor(part[:, 3, cols], gap2[:, 3, cols], up_sb[:, 3, HALF + P * c : HALF + P * c + P], ALU.mult)

        def mix(c0, n):
            cols = slice(c0, c0 + n)
            z_bf = keep.tile([P, n, PACK], BF16, name="z_bf%d" % c0, align_bytes=64)
            nc.vector.tensor_tensor(
                z_bf[:].rearrange("p (c i) t -> p c t i", i=4),
                lo[:, :, cols].rearrange("p t (c i) -> p c t i", i=4),
                part[:, :, cols].rearrange("p t (c i) -> p c t i", i=4),
                ALU.add,
            )
            return z_bf

        def quantise_z(c0, n, z_bf):
            codes = keep.tile([P, n], U32, name="z_codes%d" % c0, align_bytes=64)
            sc = keep.tile([P, n], U8, name="z_sc%d" % c0, align_bytes=64)
            nc.vector.quantize_mx(out=codes[:].bitcast(FP8X4), scales=sc[:], in_=z_bf[:].rearrange("p n t -> p (n t)"))
            return codes, sc

        def multiply(bank, b, piece, z_mx):
            codes, sc = z_mx
            for e in range(2):
                cols = slice(P * (2 * b + e), P * (2 * b + e) + P)
                nc.tensor.matmul_mx(
                    out=bank[:, e, piece],
                    lhsT=w2_codes[:, cols].bitcast(FP8X4),
                    lhsT_scale=w2_sc[:, cols],
                    rhs=codes[:].bitcast(FP8X4),
                    rhs_scale=sc[:],
                    start=True,
                    stop=True,
                )

        def finish(c0, n, z_pieces, banks):
            last = c0 + n == S
            width = n // len(z_pieces)
            tiles = [psum.tile([P, 2, n], F32, name="o_bank", tag="bank%d" % banks[b]) for b in range(2)]
            for i, z_mx in enumerate(z_pieces[:-1]):
                for b in range(2):
                    multiply(tiles[b], b, slice(width * i, width * (i + 1)), z_mx)
            for b in range(2):
                bank = tiles[b]
                multiply(bank, b, slice(n - width, n), z_pieces[-1])
                res = keep.tile([P, 2, n], F32, name="res%d_%d" % (c0, b))
                if last and b == 1:
                    nc.vector.tensor_copy(res[:], bank[:])
                else:
                    nc.scalar.copy(res[:], bank[:])
                queue = nc.scalar if last and b == 0 else nc.sync
                queue.dma_start(out[2 * P * b : 2 * P * (b + 1), c0 : c0 + n].rearrange("(e p) s -> p e s", p=P), res[:])

        quantise_w2(0)
        quantise_w2(1)
        share(0)
        share(1)
        z_mx = quantise_z(0, P, z_first[0])
        z1 = mix(0, P)
        quantise_w2(2)
        finish(0, P, [z_mx], (2, 3))
        finish(P, P, [quantise_z(P, P, z_first[1])], (4, 5))
        finish(HALF, P, [quantise_z(HALF, P, z1)], (0, 1))
        finish(HALF + P, P, [quantise_z(HALF + P, P, mix(P, P))], (6, 7))
